import numpy as np, ml_dtypes
CORES = [5,29,101,125,133,157,229,253]
N = 8
import mx_ref
BF = ml_dtypes.bfloat16
def gcols(t, e):
    v = np.concatenate([t.reshape(8, 16, -1, 4), np.zeros((8, 16, 1, 4), BF)], axis=2)
    return np.ascontiguousarray(np.stack([v[g][:, e[g]] for g in range(8)])).reshape(128, -1)
def tile(rs):
    return np.stack(rs, axis=2).reshape(128, -1).astype(BF)
def pick(q, e):
    c = np.concatenate([q[0].reshape(128, -1, 4), np.zeros((128, 1, 4), np.uint8)], axis=1); s = np.concatenate([q[1], np.ones((16, 1), np.uint8)], axis=1)
    return (np.ascontiguousarray(c[:, e].reshape(128, -1)), np.ascontiguousarray(s[:, e]))
def join(*qs):
    return (np.concatenate([q[0] for q in qs], axis=1), np.concatenate([q[1] for q in qs], axis=1))
def put(q, e, v):
    c, s = q[0].reshape(128, -1, 4).copy(), q[1].copy(); c[:, e] = v[0].reshape(128, -1, 4); s[:, e] = v[1]
    return (c.reshape(128, -1), s)
def pk(c, s):
    return (np.ascontiguousarray(c), mx_ref.live(s))
def emit(q):
    return q[0], q[1]
def packed(v, rng):
    q = [mx_ref.quantize(np.ascontiguousarray(v[r])) for r in range(N)]
    return np.stack([a for a, b in q]), np.stack([mx_ref.plane(b, rng) for a, b in q])
def values_of_codes():
    e, c = np.zeros((128, 128, 4), np.float32), np.zeros((128, 2, 4), np.uint8)
    e[np.arange(128), np.arange(128), 0] = 1
    c[:127, :, 0] = np.arange(256).reshape(2, 128).T[:127]
    return mx_ref.matmul(mx_ref.quantize(e.reshape(128, 512).astype(BF)), (c.reshape(128, 8), np.full((16, 2), 127, np.uint8))).T.reshape(-1).astype(np.float64)
CODE_VALUE, SCALE_VALUE = values_of_codes(), 2.0 ** (np.arange(256) - 127.0)
def decode(q):
    return (CODE_VALUE[q[0]].reshape(16, 8, -1, 4) * SCALE_VALUE[q[1]][:, None, :, None] + 0.0).reshape(128, -1).astype(np.float32)
def f(rng, *shape):
    return mx_ref.flush((rng.standard_normal(shape, dtype=np.float32) * np.exp2(rng.integers(-2, 3, shape[:-1] + (1,)))).astype(BF))
def wide(rng, *shape, cols=0):
    v = rng.standard_normal(shape, dtype=np.float32) * np.exp2(rng.integers(-12, 13, shape)).astype(np.float32)
    if cols: v *= np.repeat(np.exp2(rng.integers(-cols, cols + 1, shape[:-2] + (1, shape[-1] // 4))) * (rng.random(shape[:-2] + (1, shape[-1] // 4)) > 0.0625), 4, axis=-1).astype(np.float32)
    return mx_ref.flush(v.astype(BF))
C, R = 384, 2
SETS = np.arange(256)
ONE = (1 << np.arange(8))[:, None]
DECIDE = [16 * g + k for g in range(8) for k in range(10)] + [15]
def bits(b):
    return np.packbits(b, axis=-2, bitorder="little")[..., 0, :].astype(np.int64)
def numbers_of(rng):
    return {"x": np.array(f(rng, N, 128, 4 * C)), "u": np.array(f(rng, N, 128, 512)), "v": np.array(f(rng, N, 128, 512))}
def same(rng, w):
    c, s = packed(np.stack([w] * N), rng)
    return {"wc": c, "ws": np.stack([s[0]] * N)}
def weights(rng, keep=np.ones((8, 16), bool)):
    w = f(rng, 128, 2048).astype(np.float32).reshape(8, 16, 4, 8, 16, 4)
    w = np.where(keep[:, :, None, None, None, None] & keep[:, :, None], w, np.float32(0.0))
    return same(rng, w.reshape(128, 2048).astype(BF))
def setup_inputs(rng):
    return {**numbers_of(rng), **weights(rng)}
def setup_inputs_ties(rng):
    d = numbers_of(rng)
    e = rng.permutation(N)
    x = d["x"].reshape(N, 8, 16, C, 4)
    x[:, :, 0] = rng.integers(0, 3, (N, 8, C, 4)).astype(np.float32).astype(BF)
    x[e[0], 0, 0, :, 3] = 2.0
    x[e[1]] = 0.0
    u = d["u"].reshape(N, 128, 128, 4)
    u[:, :, DECIDE] = 0.0
    for g in range(8):
        u[:, 16 * g, 16 * g, 0] = 1.0
        u[:, 16 * g, 16 * g + 1, 1] = 1.0
        for k in range(8): u[:, 16 * ((g + k) % 8), 16 * g + 2 + k, 2] = 1.0
    u[:, 0, 15, 3] = 1.0
    u[e[2], 0, 15, 3] = -1.0
    keep = np.ones((8, 16), bool)
    keep[:, 0] = False
    return {"x": x.reshape(N, 128, 4 * C), "u": u.reshape(N, 128, 512), "v": d["v"], **weights(rng, keep)}
def setup_inputs_near(rng):
    d = numbers_of(rng)
    x = d["x"].astype(np.float32).reshape(N, 8, 16, C, 4)
    digits = lambda a: ((a[..., None] >> np.arange(4)) & 1) * np.exp2(np.arange(4) - 23.0)
    o = rng.permutation(N)
    n = rng.integers(0, 16, (N, 8, 3, C))
    far = []
    for r in range(N):
        if o[r] % 2 == 0:
            j, g = int(rng.integers(C)), int(rng.integers(5))
            n[r, :, 0, j] = 0
            n[r, g, 0, j] = 15
            n[r, g, 1, j] = 0
            far.append((r, j))
    have = n[:, :, 0] > n[:, :, 1]
    kind = np.where(have[:, 7], np.where(have[:, 6], 2, 1), 0)
    s = digits(2 * (7 - np.count_nonzero(have[:, :7], axis=1)) + rng.integers(0, 2, (N, C)))
    x[:, :, 8:] = 0
    x[:, 5:, :8] = 0
    x[:, :, 8:11] = digits(n)
    x[:, :, 11, :, 0] = 2.0 ** -10
    x[:, 7, 0, :, 0] = 1.0
    for k in range(2):
        x[:, k, 12] = s * (kind == k)[:, :, None]
        x[:, k, 13, :, 0] = (kind == k) * 2.0 ** -10
        x[:, 7 - k, 1, :, 0] = kind == k
    x[:, 5, 1, :, 0] = np.where(kind == 2, -(1.0 + 0.125 * rng.integers(0, 3, (N, C))) * 2.0 ** -30, 0.0)
    for r, j in far: x[r, 7, 1, j, 0] = 2.0 ** 30
    u = d["u"].reshape(N, 128, 128, 4)
    u[:, :, DECIDE] = 0.0
    for r in range(N):
        k = 2.0 ** -30 if o[r] < N // 2 else 1.0
        for g in range(8):
            for i in range(10):
                h = 16 * g + i
                u[r, 112, h, 0] = k
                u[r, 16 * g + 11, h, 0] = k
                u[r, 16 * g + 8 + i if i < 2 else 16 * ((g + i - 2) % 8) + 10, h] = k
    for p, k in ((113, 1.0), (13, 1.0), (97, 2.0 ** -30), (29, 2.0 ** -30), (81, 2.0 ** -30)): u[:, p, 15, 0] = k
    u[:, 12, 15] = 1.0
    u[:, 28, 15] = 2.0 ** -30
    keep = np.zeros((8, 16), bool)
    keep[:5, :8] = True
    return {"x": x.reshape(N, 128, 4 * C).astype(BF), "u": u.reshape(N, 128, 512), "v": d["v"], **weights(rng, keep)}
def setup_inputs_huge(rng):
    d = numbers_of(rng)
    c = rng.integers(0, 2, (N, 1, 1, C, 1)) * 2.0 - 1.0
    x = (0.9 + 0.05 * rng.random((N, 8, 16, C, 4))) * 2.0 ** 30 * c
    u = d["u"].reshape(N, 128, 128, 4)
    u[:, :, DECIDE] = 0.0
    for r in range(N):
        for h in DECIDE[:-1]: u[r, rng.permutation(128)[:64], h] = 2.0 ** 30
        u[r, :, 112] = 0.0
        u[r, :, 15] = (2.0 ** 30 * (1.0 - 0.03 * rng.random((128, 4)))).astype(np.float32).astype(BF)
    w = np.zeros((128, 4, 128, 4), np.float32)
    i = np.arange(128)
    for b in range(4): w[i, b, i, b] = -0.5
    return {"x": x.astype(np.float32).reshape(N, 128, 4 * C).astype(BF), "u": u.reshape(N, 128, 512), "v": d["v"], **same(rng, w.reshape(128, 2048).astype(BF))}
def setup_inputs_few(rng):
    d = numbers_of(rng)
    e = rng.permutation(N)
    x = d["x"].reshape(N, 8, 16, C, 4)
    k = (1.0 + (2 * rng.integers(0, 64, (N, 8, 8, C, 4)) + 1) * 2.0 ** -7) * np.exp2(-rng.integers(8, 15, (N, 8, 8, C, 4)).astype(np.float32))
    x[:, :, 8:] = (k * rng.choice([-1.0, 1.0], (N, 8, 8, C, 4))).astype(np.float32).astype(BF)
    x[:, :, 8, :, 0] = 1.96875
    have = rng.random((N, 8, C)) < 0.5
    have[e[0]] = True
    have[e[1]] = False
    have[e[2]] = np.arange(8)[:, None] == rng.integers(0, 7, C)
    j = int(rng.integers(C))
    have[e[3], 0, j] = False
    have[e[3], 1:, j] = True
    have[:, 7] = False
    x[:, :, 0, :, 0] = np.where(have, 1.0, -1.0).astype(np.float32).astype(BF)
    x[e[3], 0, 2, :, 0] = np.where(have[e[3], 0], -1.0, 1.0).astype(np.float32).astype(BF)
    s = rng.integers(-8, 9, (N, C))
    s[e[0]] = 64 + 8 * rng.integers(0, 8, C)
    s[e[0], C - 1] = 128
    x[:, 0, 1, :, 0] = s.astype(np.float32).astype(BF)
    u = d["u"].reshape(N, 128, 128, 4)
    u[:, :, ::16] = 0.0
    u[:, :, 1::16] = 0.0
    u[:, :, 15] = 0.0
    for h in range(0, 128, 16): u[:, h, h, 0] = 1.0
    u[:, 1, 15, 0] = 1.0
    u[e[3], 112, 112, 0] = 0.0
    u[e[3], 2, 112, 0] = 1.0
    u[e[3], :, 9] = 0.0
    w = f(rng, 128, 2048).astype(np.float32).reshape(8, 16, 4, 8, 16, 4)
    w[:, :, :, :, 8:] = 0
    i = np.arange(8)
    for p in range(8, 16):
        for b in range(4): w[i, p, b, i, p, b] = 32.0
    w[:, 8, 0, :, 8, 0] = 0
    w[:, :, 0, 0, 2] = 0
    w[0, 0, 0, 0, 2, 0] = -64.0
    w[:, :, 0, 7, 0] = 0
    return {"x": x.reshape(N, 128, 4 * C), "u": u.reshape(N, 128, 512), "v": d["v"], **same(rng, w.reshape(128, 2048).astype(BF))}
def setup_inputs_spread(rng):
    d = setup_inputs(rng)
    d["x"] = wide(rng, N, 128, 4 * C, cols=6)
    return d
def check_inputs(d):
    b = []
    for k in ("x", "u", "v"):
        a = np.abs(d[k].astype(np.float32))
        if not (np.isfinite(a).all() and ((a == 0) | (a >= 2.0 ** -30) & (a <= 2.0 ** 30)).all()): b.append("a value of " + k)
    if ((d["wc"] & 0x7F) == 0x7F).any(): b.append("a code of wc that is no number")
    for k in ("wc", "ws"):
        if (d[k] != d[k][:1]).any(): b.append(k + " isn't the same on all ranks")
    none, least, most = [emit(mx_ref.quantize(np.full((128, 16), k, np.float32).astype(BF)))[1][0, 0] for k in (0.0, 2.0 ** -30, 2.0 ** 30)]
    for r in range(N):
        a = mx_ref.live(d["ws"][r])
        if not ((a == none) | (a >= least) & (a <= most)).all(): b.append("a scale of ws")
    return b
def reference(x, u, v, wc, ws):
    qu = [mx_ref.quantize(u[r]) for r in range(N)]
    lay = pk(wc[0], ws[0])
    now = [x[r] for r in range(N)]
    for t in range(R):
        q = [mx_ref.quantize(now[r]) for r in range(N)]
        best, rep = np.zeros((N, 256), np.float32), np.zeros((N, 256), np.int64)
        here, want = np.zeros((N, 8, C), bool), np.zeros((N, 8, C), np.int64)
        for r in range(N):
            s = mx_ref.matmul(qu[r], q[r]) + np.float32(0.0)
            a = s.reshape(8, 16, C)
            here[r] = a[:, 0] > a[:, 1]
            m = bits(here[r])
            want[r] = (m & bits(a[:, 2:10] > a[:, 1:2])) | ONE
            holds = (m & SETS[:, None]) == SETS[:, None]
            strong = np.where(holds, s[15], np.float32(-np.inf))
            rep[r] = np.argmax(strong, axis=1)
            best[r] = np.max(strong, axis=1)
        win = np.argmax(best, axis=0)
        got = pick(join(*q), np.where(np.isfinite(best[win, SETS]), C * win + rep[win, SETS], -1))
        made = tile([mx_ref.matmul(pick(lay, np.arange(128 * b, 128 * b + 128)), got) * np.float32(0.03125) for b in range(4)])
        table = decode(mx_ref.quantize(made)).astype(BF)
        for r in range(N):
            now[r] = (now[r].astype(np.float32) + gcols(table, np.where(here[r], -1, want[r])).astype(np.float32)).astype(BF)
    y, wl = np.zeros((N, 128, C), np.float32), np.zeros((N, 8, C), np.float32)
    oc, osc = np.zeros((N, 128, 4 * C), np.uint8), np.zeros((N, 16, C), np.uint8)
    for r in range(N):
        q = mx_ref.quantize(now[r])
        y[r] = mx_ref.matmul(mx_ref.quantize(v[r]), q)
        wl[r] = want[r]
        oc[r], osc[r] = emit(q)
    return {"y": y, "wl": wl, "oc": oc, "osc": osc}

@@ -1,0 +1,486 @@
+from concourse.bass import DstId, RemoteDMATransfer
+from concourse.mybir import dt, AluOpType, ActivationFunctionType, AxisListType
+
+ALU, ACT = AluOpType, ActivationFunctionType
+NR = 8
+C = 384
+BIG = 2.0 ** 30
+
+
+def _scratch():
+    s = {}
+
+    def bf(name, n): s[name] = ("sbuf", [128, n], "bfloat16")
+    def f32(name, n): s[name] = ("sbuf", [128, n], "float32")
+    def i32(name, n): s[name] = ("sbuf", [128, n], "int32")
+    def u16(name, n): s[name] = ("sbuf", [128, n], "uint16")
+
+    def mx(name, n):
+        s[name] = ("sbuf", [128, n], "float8_e4m3fn_x4")
+        s[name + "s"] = ("sbuf", [128, n], "uint8")
+
+    bf("ut", 512); bf("vt", 512)
+    for t in range(3):
+        bf("x%d" % t, 4 * C); mx("qx%d" % t, C)
+    bf("ab", 4 * C); bf("hc", 1024); bf("zt", 512); bf("z", 1024); bf("ht", 512); bf("pr", 512)
+    bf("ct", 3584); bf("yt", 1024); bf("pf", C); bf("wf", C); bf("sj", 2 * C); bf("wzi", 512)
+    f32("pth", C); f32("ath", C); f32("s15", C); f32("mk", 2 * C); f32("ix", 2); f32("fc", 64); f32("m8", 8); f32("ni", 8)
+    f32("lf", 96); f32("yo", C); f32("wlb", C); f32("mi", 128); f32("fi", 512); f32("gw", 512); f32("et", 1024)
+    f32("wn", 32); f32("la", 24)
+    i32("ic", 16); i32("jc", 16); i32("mj", 128); i32("lu", 16); i32("ai", 16); i32("dg", 64)
+    u16("lup", 24); u16("lua", 16); u16("ls", 16); u16("off", 96)
+    mx("uq", 128); mx("up", 384); mx("ua", 256); mx("vq", 128); mx("wq", 512); mx("qab", C); mx("qhc", 256); mx("zq", 128)
+    mx("qz", 256); mx("qpr", 128); mx("qc", 896)
+    for t in range(2):
+        k = str(t)
+        f32("rm" + k, 2 * C); f32("stl" + k, 32); f32("rst" + k, 1); u16("wr" + k, 2); u16("tl" + k, 2)
+        mx("ca" + k, 128); mx("cb" + k, 128); mx("land" + k, 288); mx("tq" + k, 128); mx("qh" + k, 128); mx("yq" + k, 256)
+        mx("rp" + k, 64); mx("ry" + k, 32)
+    for b in range(8):
+        s["b%d" % b] = ("psum", [128, 512], "float32")
+    return s
+
+
+SCRATCH = _scratch()
+_REMOTE = ["st", "pc", "ps", "yco", "yso", "ycx", "ysx"]
+_RSEMS = [n + str(t) for t in range(2) for n in _REMOTE] + ["lr"]
+SEMAPHORES = _RSEMS + ["c%d" % i for i in range(135)]
+
+
+def _m(engines):
+    return sum(1 << e for e in engines)
+
+
+def _plan(T, topo):
+    cs = list(T.cores)
+    par = [0 if r == 0 or topo.may_write(cs[0], cs[r]) else 1 for r in range(NR)]
+    own = [[s for s in range(NR) if par[s] == par[r]] for r in range(NR)]
+    cross = [[s for s in range(NR) if par[s] != par[r]] for r in range(NR)]
+    kk = [own[r].index(r) for r in range(NR)]
+    relay = []
+    for r in range(NR):
+        can = [c for c in topo.cores_of(cs[r]) if c != cs[r] and all(topo.may_write(c, cs[d]) for d in cross[r])]
+        near = [c for c in can if topo.die(c) == topo.die(cs[r])]
+        far = [c for c in can if topo.die(c) != topo.die(cs[r])]
+        a, b = (near, far) if kk[r] % 2 == 0 else (far, near)
+        relay.append([(a[0], 0, 0), (b[0], 2, 0), (a[1], 0, 1), (b[1], 2, 1)])
+    return cs, par, own, cross, kk, relay
+
+
+def _dst(topo, d, core):
+    rid, pid = topo.addr(d, core)
+    return DstId(rid=rid, pnc=pid)
+
+
+def _direct(topo, r, d, cs, own):
+    o = [s for s in own[r] if s != r]
+    e = topo.engines(cs[r], cs[d])
+    i = o.index(d)
+    return (e[0:4], e[4:6], e[6:8])[i], (e[0:2], e[2:4], e[4:8])[i]
+
+
+def _relay_program(g, core, T, topo, r, first, role, plan):
+    cs, par, own, cross, kk, relay = plan
+    d0, d1 = cross[r][first], cross[r][first + 1]
+    eng = topo.engines(core, cs[d0])
+    ids = [_dst(topo, cs[d], core) for d in (d0, d1)]
+    loc = [0]
+    what = "s" if role else ""
+
+    def u8(v):
+        return v if role else v.bitcast(dt.uint8)
+
+    def send(trs, n):
+        g.remote_dma_fused(trs, local_sem=T.sem.lr)
+        loc[0] += n
+
+    for t in range(2):
+        k = str(t)
+        if role:
+            sm = T.sem["st" + k]
+            g.wait_ge(sm, 8)
+            dv = T["stl" + k][:, 4 * r:4 * r + 1]
+            send([RemoteDMATransfer(dst_ids=ids, dma_engine_mask=_m(eng), remote_sem=sm, srcs=[T["rst" + k][:]], dsts=[dv, dv])], len(eng))
+        sm = T.sem[("ps" if role else "pc") + k]
+        g.wait_ge(sm, 4)
+        half = [eng[0:4], eng[4:8]]
+        send([RemoteDMATransfer(dst_ids=[ids[i]], dma_engine_mask=_m(half[i]), remote_sem=sm, srcs=[u8(T["rp" + k + what][:, 32 * i:32 * i + 32])],
+                                dsts=[u8(T["land" + k + what][:, 32 * r:32 * r + 32])]) for i in range(2)], len(eng))
+        a = 128 * par[r] + 32 * kk[r]
+        sm = T.sem[("ysx" if role else "ycx") + k]
+        g.wait_ge(sm, 8)
+        d = T["yq" + k + what]
+        send([RemoteDMATransfer(dst_ids=ids, dma_engine_mask=_m(eng), remote_sem=sm, srcs=[u8(T["ry" + k + what][:, 0:32])],
+                                dsts=[u8(d[:, a:a + 32]), u8(d[:, a:a + 32])])], len(eng))
+    g.wait_ge(T.sem.lr, loc[0])
+
+
+def rank_program(g, core, T, topo):
+    plan = _plan(T, topo)
+    rank = T.rank_of(core)
+    if rank is None:
+        for r in range(NR):
+            for c, first, role in plan[5][r]:
+                if c == core:
+                    _relay_program(g, core, T, topo, r, first, role, plan)
+        return
+    _rank_program(g, core, T, topo, rank, plan)
+
+
+def _rank_program(g, core, T, topo, r, plan):
+    cs, par, own, cross, kk, relay = plan
+    me, mk = par[r], kk[r]
+    peers = [s for s in own[r] if s != r]
+    V, S, P = g.vector, g.scalar, g.tensor
+    names, cnt, seen, done = {}, {}, {}, {}
+    bank = [T["b%d" % i] for i in range(8)]
+    qid = {"g": g, "v": V, "s": S, "p": P, "q": g.sync}
+
+    def sem(label):
+        if label in _RSEMS:
+            return T.sem[label]
+        if label not in names:
+            names[label] = "c%d" % len(names)
+        return T.sem[names[label]]
+
+    def w(q, *labels):
+        for lb in labels:
+            n = cnt.get(lb, 0)
+            if n and seen.get((q, lb), 0) < n:
+                qid[q].wait_ge(sem(lb), n)
+                seen[(q, lb)] = n
+                done[lb] = max(done.get(lb, 0), n)
+
+    def do(q, label, deps, method, *args, **kw):
+        w(q, *deps)
+        n = kw.pop("n", 1)
+        method(*args, **kw).then_inc(sem(label), n)
+        cnt[label] = cnt.get(label, 0) + n
+
+    def dma(q, label, deps, out, in_):
+        do(q, label, deps, qid[q].dma_start, out, in_, n=16)
+
+    def ts(label, deps, out, in0, s1, op0, s2=None, op1=None):
+        if op1 is None:
+            do("v", label, deps, V.tensor_scalar, out, in0, s1, None, op0)
+        else:
+            do("v", label, deps, V.tensor_scalar, out, in0, s1, s2, op0, op1)
+
+    def mm(label, deps, out, lhs, la, rhs, ra, rb):
+        do("p", label, deps, P.matmul_mx, out, T[lhs][:, la:la + 128], T[lhs + "s"][:, la:la + 128], T[rhs][:, ra:rb], T[rhs + "s"][:, ra:rb], True, True)
+
+    def quant(label, deps, out, a, b, tile, ta):
+        do("v", label, deps, V.quantize_mx, T[out][:, a:b], T[out + "s"][:, a:b], T[tile][:, ta:ta + 4 * (b - a)])
+
+    def pick(label, deps, out, a, b, win, wa, wb, off, e, f):
+        do("v", label + "c", deps, V.tensor_copy, T[out][:, a:b].bitcast(dt.uint32), T[win][:, wa:wb].bitcast(dt.uint32).indirect(T[off][:, e:f]))
+        do("s", label + "s", deps, S.activation, T[out + "s"][:, a:b], T[win + "s"][:, wa:wb].indirect(T[off][:, e:f]), ACT.Copy)
+
+    def send(masks, deps, trs):
+        w("g", *deps)
+        g.remote_dma_fused(trs, local_sem=T.sem.lr)
+        cnt["lr"] = cnt.get("lr", 0) + sum(bin(m).count("1") for m in masks)
+
+    def u8(name, what, a, b):
+        v = T[name + what][:, a:b]
+        return v if what else v.bitcast(dt.uint8)
+
+    def iota(label, out, pattern, base, ch, whole=False):
+        if whole:
+            do("g", label, [], g.iota, out, pattern, base, ch)
+        else:
+            do("g", label, [], g.iota, out, pattern, base, ch, allow_small_or_imprecise_dtypes=True)
+
+    fc = T.fc
+
+    def F(a, n=1):
+        return fc[:, a:a + n]
+
+    dma("q", "Lu", [], T.ut[:], T.u[:])
+    dma("s", "Lx0", [], T.x0[:, 0:768], T.x[:, 0:768])
+    dma("q", "Lx1", [], T.x0[:, 768:1536], T.x[:, 768:1536])
+    dma("q", "Lw", [], T.wqs[:], T.ws[:])
+    dma("q", "Lw", [], T.wq[:].bitcast(dt.uint8), T.wc[:])
+    dma("q", "Lv", [], T.vt[:], T.v[:])
+
+    iota("gl", T.lu[:], [[1, 2], [0, 8]], 0, 16, True)
+    iota("gp", T.ic[:], [[0, 16]], 0, 1, True)
+    iota("gm", T.mi[:], [[1, 128]], 0, 0)
+    iota("gn", T.ni[:], [[1, 8]], 0, 0)
+    iota("gz", T.wzi[:], [[0, 8], [1, 16], [0, 4]], 0, 0)
+    iota("kz", T.z[:], [[0, 1024]], 0, 0)
+    iota("gf", T.fi[:], [[1, 512]], 0, 0)
+    iota("kht", T.ht[:], [[0, 512]], 0, 0)
+    iota("kht", T.pr[:, 384:512], [[0, 128]], 0, 0)
+    iota("gw", T.gw[:], [[1, 32], [0, 4], [-1, 4]], 0, 0)
+
+    do("v", "kzt", [], V.memset, T.zt[:], 0.0)
+    for i in range(3):
+        do("s", "kab", ["kzt"], S.activation, T.ab[:, 512 * i:512 * i + 512], T.zt[:], ACT.Copy)
+    do("v", "kl", [], V.memset, T.lup[:, 16:24], 15)
+    ts("kl0", ["gl"], T.lu[:], T.lu[:], 113, ALU.bitwise_and)
+    do("v", "kl", ["kl0"], V.tensor_copy, T.lup[:, 0:16], T.lu[:])
+
+    def jbits(col, shift, mask):
+        out, in0 = T.jc[:, col:col + 1], T.ic[:, 0:1]
+        if shift and mask:
+            ts("kj", ["gp"], out, in0, shift, ALU.logical_shift_right, mask, ALU.bitwise_and)
+        elif shift:
+            ts("kj", ["gp"], out, in0, shift, ALU.logical_shift_right)
+        else:
+            ts("kj", ["gp"], out, in0, mask, ALU.bitwise_and)
+
+    for col, sh, ma in ((0, 0, 7), (1, 4, 0), (2, 0, 1), (3, 4, 1), (4, 1, 1), (5, 5, 1), (6, 2, 1), (7, 6, 1), (8, 3, 1), (9, 5, 0), (10, 1, 15), (11, 0, 3), (12, 0, 127)):
+        jbits(col, sh, ma)
+    do("v", "kf", ["kj"], V.tensor_copy, fc[:, 0:13], T.jc[:, 0:13])
+    do("v", "khm", [], V.memset, T.hc[:], 0.0)
+    ts("k1", ["kf"], F(24), F(2), -0.5, ALU.mult, 1.0, ALU.add)
+    ts("k1", [], F(25), F(4), -0.75, ALU.mult, 1.0, ALU.add)
+    ts("k1", [], F(26), F(6), -0.9375, ALU.mult, 1.0, ALU.add)
+    ts("k1", [], F(29), F(9), 2.0, ALU.mult, F(2), ALU.add)
+    ts("k1", [], F(23), F(12), 7.0, ALU.is_equal)
+    ts("k1", ["k1"], F(27), F(24), F(25), ALU.mult, F(26), ALU.mult)
+    ts("k1", ["k1"], F(28), F(12), 8.0, ALU.is_lt, F(27), ALU.mult)
+    ts("k1", ["k1", "gm"], T.mi[:], T.mi[:], F(28), ALU.mult, 0.498, ALU.subtract)
+    do("v", "k1", ["k1"], V.tensor_copy, T.mj[:], T.mi[:])
+    ts("k1", ["k1"], T.mj[:], T.mj[:], 1, ALU.bitwise_and)
+    for h in range(2):
+        out = T.hc[:, 512 * h:512 * h + 512:4]
+        if (me if h else 1 - me):
+            ts("k6", ["k1", "khm"], out, T.mj[:], F(23), ALU.add, -BIG, ALU.mult)
+        else:
+            ts("k6", ["k1", "khm"], out, T.mj[:], -BIG, ALU.mult)
+    quant("uq", ["Lu"], "uq", 0, 128, "ut", 0)
+    pick("up", ["uq", "kl"], "up", 0, 384, "uq", 0, 128, "lup", 0, 24)
+    quant("qx", ["Lx0"], "qx0", 0, 192, "x0", 0)
+    quant("qx", ["Lx1"], "qx0", 192, 384, "x0", 768)
+    quant("qhc", ["k6"], "qhc", 0, 256, "hc", 0)
+    ts("kwz", ["gz"], T.ct[:, 0:512], T.wzi[:], F(10), ALU.is_equal)
+    quant("qwz", ["kwz"], "qc", 0, 128, "ct", 0)
+
+    def consts_a():
+        ts("km8", ["gn"], F(30), F(12), 4.0, ALU.mult)
+        ts("kc", [], F(31), F(2), 16.0, ALU.mult, F(10), ALU.add)
+        if me == 0 and mk == 0:
+            ts("kc", [], F(32), F(12), 0.0, ALU.is_equal, 256.0, ALU.mult)
+        else:
+            do("v", "kc", [], V.memset, F(32), 0.0)
+        for b in range(2, 4):
+            ts("ke0", ["km8"], F(53 + b), F(30), -1.0, ALU.mult, -float(b), ALU.add)
+        quant("zq", ["kzt"], "zq", 0, 128, "zt", 0)
+        for t in range(2):
+            for what in ("", "s"):
+                dma("q", "kland", ["zq"], u8("land%d" % t, what, 256, 288), u8("zq", what, 0, 32))
+                dma("q", "kland", ["zq"], u8("tq%d" % t, what, 32, 128), u8("zq", what, 32, 128))
+        for b in range(2):
+            ts("ke", ["km8", "gf"], T.ct[:, 1536 + 512 * b:2048 + 512 * b], T.fi[:], F(30), ALU.subtract, float(b), ALU.is_equal)
+        for b in range(2, 4):
+            do("s", "kea", ["ke0", "gf"], S.activation, T.et[:, 512 * b - 1024:512 * b - 512], T.fi[:], ACT.Abs, bias=F(53 + b))
+        for b in range(2, 4):
+            do("s", "kes", ["kea"], S.activation, T.ct[:, 1536 + 512 * b:2048 + 512 * b], T.et[:, 512 * b - 1024:512 * b - 512], ACT.Relu, bias=1.0, scale=-1.0)
+
+    def consts_b():
+        quant("qe", ["ke", "kes"], "qc", 384, 896, "ct", 1536)
+        ts("kn", [], F(18, 2), F(2, 2), 1.0, ALU.add)
+        ts("kn", [], F(20, 2), F(4, 2), 3.0, ALU.mult, 1.0, ALU.add)
+        ts("kn", [], F(13), F(6), 15.0, ALU.mult, 1.0, ALU.add)
+        ts("kn", [], F(14), F(7), 15.0, ALU.mult, 1.0, ALU.add)
+        ts("kn", [], F(35, 2), F(0, 2), 5.0, ALU.is_ge, 0.5, ALU.mult)
+        ts("kn", [], F(37, 2), F(0, 2), 0.0, ALU.is_equal, 15.5, ALU.mult)
+        ts("kn", [], F(44), F(0), 2.0, ALU.add)
+        ts("kn", [], F(45), F(0), F(1), ALU.not_equal)
+        ts("kn", [], F(46), F(8), -1.0, ALU.mult, 1.0, ALU.add)
+        ts("kn", [], F(54), F(1), 4.0, ALU.mult)
+        ts("kn", [], T.la[:, 0:8], T.ni[:], 16.0, ALU.mult)
+        do("v", "kn", ["kn"], V.tensor_tensor, F(33, 2), F(18, 2), F(20, 2), ALU.mult)
+        ts("kn", [], F(39, 2), F(35, 2), 0.5, ALU.add)
+        ts("kn", [], F(58, 6), T.ni[:, 0:6], F(0), ALU.not_equal, F(44), ALU.mult)
+        ts("kn", [], T.wn[:, 30:32], T.ni[:, 6:8], F(0), ALU.not_equal, F(44), ALU.mult)
+        ts("kn", [], T.la[:, 16:24], T.la[:, 0:8], 1.0, ALU.add)
+        do("v", "kn", ["kn"], V.tensor_tensor, F(16, 2), F(33, 2), F(13, 2), ALU.mult)
+        do("v", "kn", [], V.tensor_tensor, T.la[:, 8:14], F(58, 6), T.la[:, 0:6], ALU.add)
+        do("v", "kn", [], V.tensor_tensor, T.la[:, 14:16], T.wn[:, 30:32], T.la[:, 6:8], ALU.add)
+        do("v", "kn", ["kn"], V.tensor_tensor, F(41, 2), F(39, 2), F(16, 2), ALU.mult)
+        ts("kn", [], F(51), F(45), F(16), ALU.mult, F(46), ALU.mult)
+        do("v", "kla", [], V.tensor_copy, T.lua[:], T.la[:, 8:24])
+        do("v", "kn", ["kn"], V.tensor_tensor, F(47, 2), F(41, 2), F(37, 2), ALU.add)
+        ts("kn", ["kn"], F(49), F(47), 4.0, ALU.mult, 1024.0, ALU.add)
+        ts("kn", [], F(50), F(48), 4.0, ALU.mult, F(11), ALU.add)
+        ts("kn", ["kn"], F(52), F(49), F(45), ALU.mult, 1024.0, ALU.subtract)
+        ts("kn", ["kn"], F(53), F(52), F(46), ALU.mult)
+
+    def consts_c():
+        pick("ua", ["kla"], "ua", 0, 256, "uq", 0, 128, "lua", 0, 16)
+        ts("kw", ["gw", "kn"], T.ct[:, 512:1024], T.gw[:], F(54), ALU.is_equal, F(53), ALU.mult)
+        quant("qwl", ["kw"], "qc", 128, 256, "ct", 512)
+
+    def consts_d():
+        ts("kv", [], T.ct[:, 1024:1536], T.fi[:], F(54), ALU.is_equal, F(51), ALU.mult)
+        quant("qww", ["kv"], "qc", 256, 384, "ct", 1024)
+        quant("vq", ["Lv"], "vq", 0, 128, "vt", 0)
+
+    codes_to, scales_to = relay[r][0:2], relay[r][2:4]
+    e_off = topo.engines(core, cs[peers[0]])
+    e_on = [e for e in topo.engines(core, codes_to[0][0]) if e not in e_off]
+    rid = {"": [_dst(topo, c[0], core) for c in codes_to], "s": [_dst(topo, c[0], core) for c in scales_to]}
+    pid = [_dst(topo, cs[d], core) for d in peers]
+
+    for t in range(2):
+        k = str(t)
+        qx, x, xn = "qx" + k, T["x" + k], T["x%d" % (t + 1)]
+        rm = T["rm" + k]
+        mm("mpt", ["qx", "upc", "ups"], bank[1][:, 0:C], "up", 128, qx, 0, C)
+        mm("mp", [], bank[0][:, 0:C], "up", 0, qx, 0, C)
+        mm("ms", [], bank[2][:, 0:C], "up", 256, qx, 0, C)
+        do("s", "pth", ["mpt"], S.activation, T.pth[:], bank[1][:, 0:C], ACT.Copy)
+        do("s", "s15", ["ms"], S.activation, T.s15[:], bank[2][:, 0:C], ACT.Copy, scale=1.0 / BIG)
+        do("v", "pf", ["mp", "pth"], V.tensor_tensor, T.pf[:], bank[0][:, 0:C], T.pth[:], ALU.is_le)
+        ts("ab", ["pf", "kab"], T.ab[:, 0:4 * C:4], T.pf[:], BIG, ALU.mult)
+        quant("qab", ["ab"], "qab", 0, C, "ab", 0)
+        for h in range(2):
+            mm("mc%d" % h, ["qab", "qhc"], bank[5 + h][:, 0:C], "qhc", 128 * h, "qab", 0, C)
+        if t == 0:
+            ts("km8", ["gn"], T.m8[:], T.ni[:], F(29), ALU.is_equal)
+            do("v", "km8", [], V.memset, T.dg[:], 0)
+        for h in range(2):
+            hs = str(h)
+            mk_, rmh = T.mk[:, C * h:C * h + C], rm[:, C * h:C * h + C]
+            last, sj = rm[:, C * h + C - 1:C * h + C], T.sj[:, C * h:C * h + C]
+            do("v", "mk" + hs, ["mc" + hs, "s15"], V.tensor_tensor, mk_, bank[5 + h][:, 0:C], T.s15[:], ALU.add)
+            do("v", "rm" + hs, ["mk" + hs], V.tensor_tensor_scan, rmh, mk_, mk_, -1e29, ALU.max, ALU.max)
+            do("s", "ix" + hs, ["rm" + hs], S.activation, sj, rmh, ACT.Sign, bias=last, scale=-1.0, accum_out=T.ix[:, h:h + 1])
+        send([_m(e_on)], ["rm0"], [RemoteDMATransfer(dst_ids=rid["s"], dma_engine_mask=_m(e_on), remote_sem=T.sem["st" + k], srcs=[rm[:, C - 1:C]], dsts=[T["rst" + k][:], T["rst" + k][:]])])
+        send([_m(e_off)], ["rm1"], [RemoteDMATransfer(dst_ids=pid, dma_engine_mask=_m(e_off), remote_sem=T.sem["st" + k], srcs=[rm[:, 2 * C - 1:2 * C]],
+                                                      dsts=[T["stl" + k][:, 4 * r:4 * r + 1] for d in peers])])
+
+        def digits(h):
+            hs, ai = str(h), T.ai[:, 8 * h:8 * h + 8]
+            ts("da" + hs, ["ix" + hs, "km8"], ai, T.m8[:], T.ix[:, h:h + 1], ALU.mult)
+            for b, ma in enumerate((448, 56, 7)):
+                ts("db" + hs, ["da" + hs], T.dg[:, 32 * h + b:32 * h + 32:4], ai, ma, ALU.bitwise_and)
+
+        def spread(h):
+            hs = str(h)
+            do("v", "dz" + hs, ["db" + hs, "kz"], V.tensor_copy, T.z[:, 512 * h:512 * h + 32], T.dg[:, 32 * h:32 * h + 32])
+            quant("qz" + hs, ["dz" + hs], "qz", 128 * h, 128 * h + 128, "z", 512 * h)
+            mm("mz" + hs, ["qz" + hs, "qwz"], bank[(7, 0)[h]][:, 0:128], "qc", 0, "qz", 128 * h, 128 * h + 128)
+
+        def choose(h):
+            hs = str(h)
+            do("v", "ls" + hs, ["mz" + hs], V.tensor_copy, T.ls[:, 8 * h:8 * h + 8], bank[(7, 0)[h]][:, 0:8])
+            pick("c" + hs, ["ls" + hs], ("ca", "cb")[h] + k, 0, 128, qx, 0, C, "ls", 8 * h, 8 * h + 8)
+
+        digits(0)
+        spread(0)
+        digits(1)
+        choose(0)
+        spread(1)
+        choose(1)
+        for what, sm, lb in (("", "pc", "c0c"), ("s", "ps", "c0s")):
+            ms = [_m(e_on[0:4]), _m(e_on[4:8])]
+            send(ms, [lb], [RemoteDMATransfer(dst_ids=[rid[what][i]], dma_engine_mask=ms[i], remote_sem=T.sem[sm + k],
+                                              srcs=[u8("ca" + k, what, 32 * codes_to[i][1], 32 * codes_to[i][1] + 64)], dsts=[u8("rp" + k, what, 0, 64)]) for i in range(2)])
+        for what, sm, lb in (("", "pc", "c1c"), ("s", "ps", "c1s")):
+            ms = [_m(_direct(topo, r, d, cs, own)[1 if what else 0]) for d in peers]
+            send(ms, [lb], [RemoteDMATransfer(dst_ids=[pid[i]], dma_engine_mask=ms[i], remote_sem=T.sem[sm + k],
+                                              srcs=[u8("cb" + k, what, 32 * kk[d], 32 * kk[d] + 32)], dsts=[u8("land" + k, what, 32 * r, 32 * r + 32)]) for i, d in enumerate(peers)])
+        for what, lb in (("", "c1c"), ("s", "c1s")):
+            dma("q", "cown" + what, [lb], u8("land" + k, what, 32 * r, 32 * r + 32), u8("cb" + k, what, 32 * mk, 32 * mk + 32))
+        do("v", "sown", ["rm1"], V.tensor_copy, T["stl" + k][:, 4 * r:4 * r + 1], rm[:, 2 * C - 1:2 * C])
+
+        def wishes():
+            mm("ma", ["uac", "uas", "pth", "ls1"], bank[1][:, 0:C], "ua", 0, qx, 0, C)
+            mm("mat", ["s15"], bank[2][:, 0:C], "ua", 128, qx, 0, C)
+            do("s", "ath", ["mat"], S.activation, T.ath[:], bank[2][:, 0:C], ACT.Copy)
+            do("v", "wf", ["ma", "ath"], V.tensor_tensor, T.wf[:], bank[1][:, 0:C], T.ath[:], ALU.is_gt)
+            do("v", "pr", ["wf", "kht"], V.tensor_tensor, T.pr[:, 0:C], T.wf[:], T.pf[:], ALU.is_gt)
+            quant("qpr", ["pr"], "qpr", 0, 128, "pr", 0)
+            mm("ml", ["qpr", "qwl", "ls1"], bank[0][:, 0:128], "qc", 128, "qpr", 0, 128)
+            ts("lf", ["ml"], T.lf[:], bank[0][:, 0:96], F(50), ALU.add)
+            do("v", "off", ["lf"], V.tensor_copy, T.off[:], T.lf[:])
+
+        if t == 0:
+            consts_a()
+        else:
+            wishes()
+        cnt["st" + k] = 8 * 3 + 8 * 4
+        wn, so = T.wn, T["stl" + k]
+        do("v", "w1", ["st" + k, "sown"], V.tensor_tensor_scan, wn[:, 0:8], so[:, 0:32:4], so[:, 0:32:4], -1e29, ALU.max, ALU.max)
+        ts("w1", ["w1"], wn[:, 8:16], wn[:, 0:8], wn[:, 7:8], ALU.is_lt)
+        ts("w1", [], wn[:, 18:19], wn[:, 7:8], -2.0 ** 50, ALU.is_lt, 256.0, ALU.mult)
+        do("v", "w1", ["w1"], V.tensor_reduce, wn[:, 16:17], wn[:, 8:16], AxisListType.X, ALU.add)
+        ts("w1", ["w1", "kc"], wn[:, 17:18], wn[:, 16:17], 32.0, ALU.mult, F(31), ALU.add)
+        ts("w1", ["w1"], wn[:, 19:20], wn[:, 17:18], wn[:, 18:19], ALU.max, F(32), ALU.max)
+        do("v", "w6", ["w1"], V.tensor_copy, T["wr" + k][:, 0:1], wn[:, 19:20])
+        for gg in range(8):
+            dma("q" if gg % 2 == 0 else "s", "tl", ["w6"], T["tl" + k][16 * gg:16 * gg + 16, 0:2], T["wr" + k][32 * mk:32 * mk + 32, 0:1])
+        if t == 0:
+            consts_b()
+        else:
+            consts_d()
+        cnt["pc" + k] = sum(len(_direct(topo, s, r, cs, own)[0]) for s in peers) + 16
+        cnt["ps" + k] = sum(len(_direct(topo, s, r, cs, own)[1]) for s in peers) + 16
+        win, tq = "land" + k, "tq" + k
+        w("v", "tl", "kland", "cown", "pc" + k)
+        w("s", "tl", "kland", "cowns", "ps" + k)
+        pick("t", [], tq, 0, 32, win, 0, 288, "tl" + k, 0, 2)
+        for b in range(4):
+            mm("mh%d" % b, ["tc", "ts", "Lw"], bank[3 + b][:, 0:128], "wq", 128 * b, tq, 0, 128)
+            if b % 2 == 0:
+                ts("hv", ["mh%d" % b, "kht"], T.ht[:, b:128:4], bank[3 + b][:, 0:32], 0.03125, ALU.mult)
+            else:
+                do("s", "hs", ["mh%d" % b, "kht"], S.activation, T.ht[:, b:128:4], bank[3 + b][:, 0:32], ACT.Copy, scale=0.03125)
+        qh = "qh" + k
+        quant("qh", ["hv", "hs"], qh, 0, 128, "ht", 0)
+        a = 128 * me + 32 * mk
+        for what, so_, sx in (("", "yco", "ycx"), ("s", "yso", "ysx")):
+            ms = [_m(e_off), _m(e_on)]
+            send(ms, ["qh"], [
+                RemoteDMATransfer(dst_ids=rid[what], dma_engine_mask=ms[1], remote_sem=T.sem[sx + k], srcs=[u8(qh, what, 0, 32)], dsts=[u8("ry" + k, what, 0, 32) for i in range(2)]),
+                RemoteDMATransfer(dst_ids=pid, dma_engine_mask=ms[0], remote_sem=T.sem[so_ + k], srcs=[u8(qh, what, 0, 32)], dsts=[u8("yq" + k, what, a, a + 32) for d in peers])])
+            dma("q", "yown", ["qh"], u8("yq" + k, what, a, a + 32), u8(qh, what, 0, 32))
+        if t == 0:
+            consts_c()
+            wishes()
+        else:
+            do("v", "pw", ["pr"], V.tensor_copy, T.ab[:, 0:4 * C:4], T.pr[:, 0:C])
+            quant("qpw", ["pw"], "qab", 0, C, "ab", 0)
+            mm("mw", ["qpw", "qww"], bank[7][:, 0:C], "qc", 256, "qab", 0, C)
+            ts("wlb", ["mw"], T.wlb[0:8, :], bank[7][0:8, 0:C], fc[0:8, 16:17], ALU.add)
+            dma("q", "swl", ["wlb"], T.wl[:], T.wlb[0:8, :])
+        cnt["yco" + k] = cnt["yso" + k] = 24
+        cnt["ycx" + k] = cnt["ysx" + k] = 32
+        for i, (half, bb, deps) in enumerate(((me, (3, 4, 5, 6), ["qh", "qe", "yown", "yco" + k, "yso" + k]),
+                                              (1 - me, (1, 2, 7, 0), ["wf", "ath", "wlb", "lf", "ls0", "ycx" + k, "ysx" + k]))):
+            for b in range(4):
+                lb = ("mh%d" if i == 0 else "md%d") % b
+                mm(lb, deps, bank[bb[b]][:, 0:128], "qc", 384 + 128 * b, "yq" + k, 128 * half, 128 * half + 128)
+                out = T.yt[:, 512 * half + b:512 * half + 512:4]
+                if b % 2 == 0:
+                    do("v", "yv", [lb], V.tensor_copy, out, bank[bb[b]][:, 0:128])
+                else:
+                    do("s", "ys", [lb], S.activation, out, bank[bb[b]][:, 0:128], ACT.Copy)
+        step = (1, 3)[t]
+        n = C // step
+        for c in range(step):
+            do("v", "xn%d" % c, ["yv", "ys", "off", "qx"], V.tensor_tensor, xn[:, 4 * n * c:4 * n * (c + 1)],
+               T.yt[:, 0:1024].indirect(T.off[:, n // 4 * c:n // 4 * (c + 1)]), x[:, 4 * n * c:4 * n * (c + 1)], ALU.add)
+            if c:
+                quant("qy%d" % (c - 1), ["xn%d" % (c - 1)], "qx2", n * (c - 1), n * c, "x2", 4 * n * (c - 1))
+        quant("qx" if t == 0 else "qy2", ["xn%d" % (step - 1)], "qx%d" % (t + 1), C - n, C, "x%d" % (t + 1), 4 * (C - n))
+
+    for c in range(3):
+        a, b = 128 * c, 128 * c + 128
+        mm("my%d" % c, ["qy%d" % c, "vq"], bank[3 + c][:, 0:128], "vq", 0, "qx2", a, b)
+        if c < 2:
+            do("s", "yo%d" % c, ["my%d" % c], S.activation, T.yo[:, a:b], bank[3 + c][:, 0:128], ACT.Copy)
+        else:
+            do("v", "yo%d" % c, ["my%d" % c], V.tensor_copy, T.yo[:, a:b], bank[3 + c][:, 0:128])
+        dma("q", "so", ["qy%d" % c], T.oc[:, 4 * a:4 * b], T.qx2[:, a:b].bitcast(dt.uint8))
+        dma("q", "so", ["yo%d" % c], T.y[:, a:b], T.yo[:, a:b])
+    for i in range(4):
+        dma("s", "ss", ["qy0", "qy1", "qy2"], T.osc[4 * i:4 * i + 4, :], T.qx2s[32 * i:32 * i + 4, :])
+    w("s", "ss")
+    for lb in list(cnt):
+        if done.get(lb, 0) < cnt[lb]:
+            w("g" if lb == "lr" else "q", lb)

@@ -26,14 +26,14 @@ def _scratch():
     bf("ct", 3584); bf("yt", 1024); bf("pf", C); bf("wf", C); bf("sj", 2 * C); bf("wzi", 512)
     f32("pth", C); f32("ath", C); f32("s15", C); f32("mk", 2 * C); f32("ix", 2); f32("fc", 64); f32("m8", 8); f32("ni", 8)
     f32("lf", 96); f32("yo", C); f32("wlb", C); f32("mi", 128); f32("fi", 512); f32("gw", 512); f32("et", 1024)
-    f32("wn", 32); f32("la", 24)
+    f32("wn", 32); f32("wt", 128); f32("wm", 32); f32("wi", 32); f32("la", 24)
     i32("ic", 16); i32("jc", 16); i32("mj", 128); i32("lu", 16); i32("ai", 16); i32("dg", 64)
     u16("lup", 24); u16("lua", 16); u16("ls", 16); u16("off", 96)
     mx("uq", 128); mx("up", 384); mx("ua", 256); mx("vq", 128); mx("wq", 512); mx("qab", C); mx("qhc", 256); mx("zq", 128)
     mx("qz", 256); mx("qpr", 128); mx("qc", 896)
     for t in range(2):
         k = str(t)
-        f32("rm" + k, 2 * C); f32("stl" + k, 32); f32("rst" + k, 1); u16("wr" + k, 2); u16("tl" + k, 2)
+        f32("rm" + k, 2 * C); f32("stl" + k, 32); f32("rst" + k, 1); u16("tl" + k, 2)
         mx("ca" + k, 128); mx("cb" + k, 128); mx("land" + k, 288); mx("tq" + k, 128); mx("qh" + k, 128); mx("yq" + k, 256)
         mx("rp" + k, 64); mx("ry" + k, 32)
     for b in range(8):
@@ -96,19 +96,17 @@ def _relay_program(g, core, T, topo, r, first, role, plan):
 
     for t in range(2):
         k = str(t)
-        if role:
-            sm = T.sem["st" + k]
-            g.wait_ge(sm, 8)
-            dv = T["stl" + k][:, 4 * r:4 * r + 1]
-            send([RemoteDMATransfer(dst_ids=ids, dma_engine_mask=_m(eng), remote_sem=sm, srcs=[T["rst" + k][:]], dsts=[dv, dv])], len(eng))
+        sm = T.sem["st" + k]
+        g.wait_ge(sm, 8)
+        send([RemoteDMATransfer(dst_ids=[ids[role]], dma_engine_mask=_m(eng), remote_sem=sm, srcs=[T["rst" + k][:]], dsts=[T["stl" + k][:, 4 * r:4 * r + 1]])], len(eng))
         sm = T.sem[("ps" if role else "pc") + k]
-        g.wait_ge(sm, 4)
+        g.wait_ge(sm, 8)
         half = [eng[0:4], eng[4:8]]
         send([RemoteDMATransfer(dst_ids=[ids[i]], dma_engine_mask=_m(half[i]), remote_sem=sm, srcs=[u8(T["rp" + k + what][:, 32 * i:32 * i + 32])],
                                 dsts=[u8(T["land" + k + what][:, 32 * r:32 * r + 32])]) for i in range(2)], len(eng))
         a = 128 * par[r] + 32 * kk[r]
         sm = T.sem[("ysx" if role else "ycx") + k]
-        g.wait_ge(sm, 8)
+        g.wait_ge(sm, 8 if role else 16)
         d = T["yq" + k + what]
         send([RemoteDMATransfer(dst_ids=ids, dma_engine_mask=_m(eng), remote_sem=sm, srcs=[u8(T["ry" + k + what][:, 0:32])],
                                 dsts=[u8(d[:, a:a + 32]), u8(d[:, a:a + 32])])], len(eng))
@@ -176,6 +174,9 @@ def _rank_program(g, core, T, topo, r, plan):
         do("v", label + "c", deps, V.tensor_copy, T[out][:, a:b].bitcast(dt.uint32), T[win][:, wa:wb].bitcast(dt.uint32).indirect(T[off][:, e:f]))
         do("s", label + "s", deps, S.activation, T[out + "s"][:, a:b], T[win + "s"][:, wa:wb].indirect(T[off][:, e:f]), ACT.Copy)
 
+    def act(label, deps, out, in_, func=ACT.Copy, **kw):
+        do("s", label, deps, S.activation, out, in_, func, **kw)
+
     def send(masks, deps, trs):
         w("g", *deps)
         g.remote_dma_fused(trs, local_sem=T.sem.lr)
@@ -199,7 +200,7 @@ def _rank_program(g, core, T, topo, r, plan):
     dma("q", "Lu", [], T.ut[:], T.u[:])
     dma("s", "Lx0", [], T.x0[:, 0:768], T.x[:, 0:768])
     dma("q", "Lx1", [], T.x0[:, 768:1536], T.x[:, 768:1536])
-    dma("q", "Lw", [], T.wqs[:], T.ws[:])
+    dma("q", "Lw", ["Lx0", "Lx1"], T.wqs[:], T.ws[:])
     dma("q", "Lw", [], T.wq[:].bitcast(dt.uint8), T.wc[:])
     dma("q", "Lv", [], T.vt[:], T.v[:])
 
@@ -210,77 +211,90 @@ def _rank_program(g, core, T, topo, r, plan):
     iota("gz", T.wzi[:], [[0, 8], [1, 16], [0, 4]], 0, 0)
     iota("kz", T.z[:], [[0, 1024]], 0, 0)
     iota("gf", T.fi[:], [[1, 512]], 0, 0)
-    iota("kht", T.ht[:], [[0, 512]], 0, 0)
-    iota("kht", T.pr[:, 384:512], [[0, 128]], 0, 0)
-    iota("gw", T.gw[:], [[1, 32], [0, 4], [-1, 4]], 0, 0)
+    iota("gf", T.wi[:], [[1, 16], [0, 2]], 0, 0)
+    iota("gf", T.gw[:], [[1, 32], [0, 4], [-1, 4]], 0, 0)
 
     do("v", "kzt", [], V.memset, T.zt[:], 0.0)
-    for i in range(3):
-        do("s", "kab", ["kzt"], S.activation, T.ab[:, 512 * i:512 * i + 512], T.zt[:], ACT.Copy)
+    for i in range(2):
+        act("khm", ["kzt"], T.hc[:, 512 * i:512 * i + 512], T.zt[:])
+    for i in range(2):
+        act("kab", [], T.ab[:, 512 * i:512 * i + 512], T.zt[:])
     do("v", "kl", [], V.memset, T.lup[:, 16:24], 15)
-    ts("kl0", ["gl"], T.lu[:], T.lu[:], 113, ALU.bitwise_and)
-    do("v", "kl", ["kl0"], V.tensor_copy, T.lup[:, 0:16], T.lu[:])
+    ts("kl", ["gl"], T.lu[:], T.lu[:], 113, ALU.bitwise_and)
+    do("v", "kl", ["kl"], V.tensor_copy, T.lup[:, 0:16], T.lu[:])
 
-    def jbits(col, shift, mask):
-        out, in0 = T.jc[:, col:col + 1], T.ic[:, 0:1]
-        if shift and mask:
-            ts("kj", ["gp"], out, in0, shift, ALU.logical_shift_right, mask, ALU.bitwise_and)
-        elif shift:
-            ts("kj", ["gp"], out, in0, shift, ALU.logical_shift_right)
-        else:
-            ts("kj", ["gp"], out, in0, mask, ALU.bitwise_and)
+    def jbits(*specs):
+        for col, shift, mask in specs:
+            out, in0 = T.jc[:, col:col + 1], T.ic[:, 0:1]
+            if shift and mask:
+                ts("kj", ["gp"], out, in0, shift, ALU.logical_shift_right, mask, ALU.bitwise_and)
+            elif shift:
+                ts("kj", ["gp"], out, in0, shift, ALU.logical_shift_right)
+            else:
+                ts("kj", ["gp"], out, in0, mask, ALU.bitwise_and)
 
-    for col, sh, ma in ((0, 0, 7), (1, 4, 0), (2, 0, 1), (3, 4, 1), (4, 1, 1), (5, 5, 1), (6, 2, 1), (7, 6, 1), (8, 3, 1), (9, 5, 0), (10, 1, 15), (11, 0, 3), (12, 0, 127)):
-        jbits(col, sh, ma)
-    do("v", "kf", ["kj"], V.tensor_copy, fc[:, 0:13], T.jc[:, 0:13])
-    do("v", "khm", [], V.memset, T.hc[:], 0.0)
-    ts("k1", ["kf"], F(24), F(2), -0.5, ALU.mult, 1.0, ALU.add)
-    ts("k1", [], F(25), F(4), -0.75, ALU.mult, 1.0, ALU.add)
-    ts("k1", [], F(26), F(6), -0.9375, ALU.mult, 1.0, ALU.add)
+    jbits((0, 0, 7), (2, 0, 1), (4, 1, 1), (6, 2, 1), (9, 5, 0), (10, 1, 15))
+    do("v", "kf", ["kj"], V.tensor_copy, fc[:, 0:8:2], T.jc[:, 0:8:2])
+    do("v", "kf", [], V.tensor_copy, fc[:, 9:11], T.jc[:, 9:11])
+    ts("k1", ["kf"], F(24), F(2), -1.0, ALU.mult, 2.0, ALU.add)
+    ts("k1", [], F(25), F(4), -3.0, ALU.mult, 4.0, ALU.add)
+    ts("k1", [], F(26), F(6), -15.0, ALU.mult, 16.0, ALU.add)
     ts("k1", [], F(29), F(9), 2.0, ALU.mult, F(2), ALU.add)
-    ts("k1", [], F(23), F(12), 7.0, ALU.is_equal)
+    ts("k1", [], F(23), F(0), 7.0, ALU.is_equal, 128.0, ALU.mult)
+    ts("k1", [], F(57), F(10), -1.0, ALU.mult)
     ts("k1", ["k1"], F(27), F(24), F(25), ALU.mult, F(26), ALU.mult)
-    ts("k1", ["k1"], F(28), F(12), 8.0, ALU.is_lt, F(27), ALU.mult)
-    ts("k1", ["k1", "gm"], T.mi[:], T.mi[:], F(28), ALU.mult, 0.498, ALU.subtract)
-    do("v", "k1", ["k1"], V.tensor_copy, T.mj[:], T.mi[:])
-    ts("k1", ["k1"], T.mj[:], T.mj[:], 1, ALU.bitwise_and)
+    ts("k1", ["k1", "gm"], T.mj[:], T.mi[:], F(27), ALU.mult)
+    ts("k1", ["k1"], T.mj[:], T.mj[:], 128, ALU.bitwise_and)
+    w("v", "k1", "khm")
     for h in range(2):
         out = T.hc[:, 512 * h:512 * h + 512:4]
         if (me if h else 1 - me):
-            ts("k6", ["k1", "khm"], out, T.mj[:], F(23), ALU.add, -BIG, ALU.mult)
+            ts("k1", [], out, T.mj[:], F(23), ALU.add, -BIG / 128, ALU.mult)
         else:
-            ts("k6", ["k1", "khm"], out, T.mj[:], -BIG, ALU.mult)
+            ts("k1", [], out, T.mj[:], -BIG / 128, ALU.mult)
     quant("uq", ["Lu"], "uq", 0, 128, "ut", 0)
-    pick("up", ["uq", "kl"], "up", 0, 384, "uq", 0, 128, "lup", 0, 24)
-    quant("qx", ["Lx0"], "qx0", 0, 192, "x0", 0)
-    quant("qx", ["Lx1"], "qx0", 192, 384, "x0", 768)
-    quant("qhc", ["k6"], "qhc", 0, 256, "hc", 0)
-    ts("kwz", ["gz"], T.ct[:, 0:512], T.wzi[:], F(10), ALU.is_equal)
-    quant("qwz", ["kwz"], "qc", 0, 128, "ct", 0)
+    pick("up", ["uq", "kl"], "up", 0, 256, "uq", 0, 128, "lup", 0, 16)
+    quant("qx0", ["Lx0"], "qx0", 0, 192, "x0", 0)
+    quant("qx1", ["Lx1"], "qx0", 192, 384, "x0", 768)
+    act("kab", [], T.ab[:, 1024:1536], T.zt[:])
+    pick("u5", [], "up", 256, 384, "uq", 0, 128, "lup", 16, 24)
+    quant("qhc", ["k1"], "qhc", 0, 256, "hc", 0)
+    quant("zq", ["kzt"], "zq", 0, 128, "zt", 0)
+    for t in range(2):
+        for what in ("", "s"):
+            dma("q", "kland", ["zq"], u8("land%d" % t, what, 256, 288), u8("zq", what, 0, 32))
+            dma("q", "kland", ["zq"], u8("tq%d" % t, what, 32, 128), u8("zq", what, 32, 128))
 
     def consts_a():
-        ts("km8", ["gn"], F(30), F(12), 4.0, ALU.mult)
+        jbits((1, 4, 0), (3, 4, 1), (5, 5, 1), (7, 6, 1), (8, 3, 1), (11, 0, 3), (12, 0, 127), (14, 0, 15))
+        do("v", "kf", ["kj"], V.tensor_copy, fc[:, 1:8:2], T.jc[:, 1:8:2])
+        do("v", "kf", [], V.tensor_copy, F(8), T.jc[:, 8:9])
+        do("v", "kf", [], V.tensor_copy, F(11, 2), T.jc[:, 11:13])
+        do("v", "kf", [], V.tensor_copy, F(22), T.jc[:, 14:15])
+        ts("km8", ["kf"], F(30), F(12), 4.0, ALU.mult)
         ts("kc", [], F(31), F(2), 16.0, ALU.mult, F(10), ALU.add)
         if me == 0 and mk == 0:
-            ts("kc", [], F(32), F(12), 0.0, ALU.is_equal, 256.0, ALU.mult)
+            ts("kwt", [], F(15), F(12), 0.0, ALU.is_equal, 2.0 ** 81, ALU.mult)
+            ts("kc", ["kwt"], F(32), F(15), -2.0 ** 50, ALU.add)
         else:
-            do("v", "kc", [], V.memset, F(32), 0.0)
-        for b in range(2, 4):
-            ts("ke0", ["km8"], F(53 + b), F(30), -1.0, ALU.mult, -float(b), ALU.add)
-        quant("zq", ["kzt"], "zq", 0, 128, "zt", 0)
-        for t in range(2):
-            for what in ("", "s"):
-                dma("q", "kland", ["zq"], u8("land%d" % t, what, 256, 288), u8("zq", what, 0, 32))
-                dma("q", "kland", ["zq"], u8("tq%d" % t, what, 32, 128), u8("zq", what, 32, 128))
-        for b in range(2):
-            ts("ke", ["km8", "gf"], T.ct[:, 1536 + 512 * b:2048 + 512 * b], T.fi[:], F(30), ALU.subtract, float(b), ALU.is_equal)
-        for b in range(2, 4):
-            do("s", "kea", ["ke0", "gf"], S.activation, T.et[:, 512 * b - 1024:512 * b - 512], T.fi[:], ACT.Abs, bias=F(53 + b))
-        for b in range(2, 4):
-            do("s", "kes", ["kea"], S.activation, T.ct[:, 1536 + 512 * b:2048 + 512 * b], T.et[:, 512 * b - 1024:512 * b - 512], ACT.Relu, bias=1.0, scale=-1.0)
+            do("v", "kc", [], V.memset, F(32), -2.0 ** 50)
+        do("v", "kwt", [], V.memset, T.wt[:, 0:32], 0.0)
+        ts("kwt", ["gf"], T.wm[:], T.wi[:], F(22), ALU.is_equal)
+        for b in range(4):
+            ts("ke0", ["km8"], F((28, 43, 55, 56)[b]), F(30), -1.0, ALU.mult, -float(b), ALU.add)
+        do("v", "kht", [], V.memset, T.ht[:], 0.0)
+        do("v", "kht", [], V.memset, T.pr[:, 384:512], 0.0)
+        unpackers(2)
+        unpackers(3)
 
-    def consts_b():
-        quant("qe", ["ke", "kes"], "qc", 384, 896, "ct", 1536)
+    def unpackers(b, stage=2):
+        e = T.et[:, 512 * (b % 2):512 * (b % 2) + 512]
+        if stage != 1:
+            act("kes", ["ke0", "gf"], e, T.fi[:], ACT.Abs, bias=F((28, 43, 55, 56)[b]))
+        if stage:
+            act("kes", ["kes"], T.ct[:, 1536 + 512 * b:2048 + 512 * b], e, ACT.Relu, bias=1.0, scale=-1.0)
+
+    def consts_b1():
         ts("kn", [], F(18, 2), F(2, 2), 1.0, ALU.add)
         ts("kn", [], F(20, 2), F(4, 2), 3.0, ALU.mult, 1.0, ALU.add)
         ts("kn", [], F(13), F(6), 15.0, ALU.mult, 1.0, ALU.add)
@@ -292,11 +306,15 @@ def _rank_program(g, core, T, topo, r, plan):
         ts("kn", [], F(46), F(8), -1.0, ALU.mult, 1.0, ALU.add)
         ts("kn", [], F(54), F(1), 4.0, ALU.mult)
         ts("kn", [], T.la[:, 0:8], T.ni[:], 16.0, ALU.mult)
+
+    def consts_b2():
         do("v", "kn", ["kn"], V.tensor_tensor, F(33, 2), F(18, 2), F(20, 2), ALU.mult)
         ts("kn", [], F(39, 2), F(35, 2), 0.5, ALU.add)
         ts("kn", [], F(58, 6), T.ni[:, 0:6], F(0), ALU.not_equal, F(44), ALU.mult)
         ts("kn", [], T.wn[:, 30:32], T.ni[:, 6:8], F(0), ALU.not_equal, F(44), ALU.mult)
         ts("kn", [], T.la[:, 16:24], T.la[:, 0:8], 1.0, ALU.add)
+
+    def consts_b3():
         do("v", "kn", ["kn"], V.tensor_tensor, F(16, 2), F(33, 2), F(13, 2), ALU.mult)
         do("v", "kn", [], V.tensor_tensor, T.la[:, 8:14], F(58, 6), T.la[:, 0:6], ALU.add)
         do("v", "kn", [], V.tensor_tensor, T.la[:, 14:16], T.wn[:, 30:32], T.la[:, 6:8], ALU.add)
@@ -311,7 +329,7 @@ def _rank_program(g, core, T, topo, r, plan):
 
     def consts_c():
         pick("ua", ["kla"], "ua", 0, 256, "uq", 0, 128, "lua", 0, 16)
-        ts("kw", ["gw", "kn"], T.ct[:, 512:1024], T.gw[:], F(54), ALU.is_equal, F(53), ALU.mult)
+        ts("kw", ["gf", "kn"], T.ct[:, 512:1024], T.gw[:], F(54), ALU.is_equal, F(53), ALU.mult)
         quant("qwl", ["kw"], "qc", 128, 256, "ct", 512)
 
     def consts_d():
@@ -329,27 +347,48 @@ def _rank_program(g, core, T, topo, r, plan):
         k = str(t)
         qx, x, xn = "qx" + k, T["x" + k], T["x%d" % (t + 1)]
         rm = T["rm" + k]
-        mm("mpt", ["qx", "upc", "ups"], bank[1][:, 0:C], "up", 128, qx, 0, C)
-        mm("mp", [], bank[0][:, 0:C], "up", 0, qx, 0, C)
-        mm("ms", [], bank[2][:, 0:C], "up", 256, qx, 0, C)
-        do("s", "pth", ["mpt"], S.activation, T.pth[:], bank[1][:, 0:C], ACT.Copy)
-        do("s", "s15", ["ms"], S.activation, T.s15[:], bank[2][:, 0:C], ACT.Copy, scale=1.0 / BIG)
-        do("v", "pf", ["mp", "pth"], V.tensor_tensor, T.pf[:], bank[0][:, 0:C], T.pth[:], ALU.is_le)
-        ts("ab", ["pf", "kab"], T.ab[:, 0:4 * C:4], T.pf[:], BIG, ALU.mult)
-        quant("qab", ["ab"], "qab", 0, C, "ab", 0)
+        for i in range(2):
+            lo, hi = 192 * i, 192 * i + 192
+            mm("mpt%d" % i, ["qx%d" % i, "upc", "ups"], bank[(1, 4)[i]][:, 0:192], "up", 128, qx, lo, hi)
+            mm("mp%d" % i, [], bank[(0, 3)[i]][:, 0:192], "up", 0, qx, lo, hi)
+            act("pth%d" % i, ["mpt%d" % i], T.pth[:, lo:hi], bank[(1, 4)[i]][:, 0:192])
+        mm("ms", ["u5c", "u5s"], bank[2][:, 0:C], "up", 256, qx, 0, C)
+        act("s15", ["ms"], T.s15[:], bank[2][:, 0:C], scale=1.0 / BIG)
+        if t == 0:
+            act("kwz", ["gz", "k1"], T.et[:, 0:512], T.wzi[:], ACT.Abs, bias=F(57))
+            act("kwz", ["kwz"], T.ct[:, 0:512], T.et[:, 0:512], ACT.Relu, bias=1.0, scale=-1.0)
+        for i in range(2):
+            lo, hi = 192 * i, 192 * i + 192
+            do("v", "pf%d" % i, ["mp%d" % i, "pth%d" % i], V.tensor_tensor, T.pf[:, lo:hi], bank[(0, 3)[i]][:, 0:192], T.pth[:, lo:hi], ALU.is_le)
+            if i:
+                quant("qab", ["ab"], "qab", 0, 192, "ab", 0)
+            ts("ab", ["pf%d" % i, "kab"], T.ab[:, 4 * lo:4 * hi:4], T.pf[:, lo:hi], BIG, ALU.mult)
+        quant("qab", ["ab"], "qab", 192, 384, "ab", 768)
         for h in range(2):
             mm("mc%d" % h, ["qab", "qhc"], bank[5 + h][:, 0:C], "qhc", 128 * h, "qab", 0, C)
+
+        def scores():
+            mm("ma", ["uac", "uas", "pth0", "pth1"], bank[1][:, 0:C], "ua", 0, qx, 0, C)
+            mm("mat", ["s15"], bank[2][:, 0:C], "ua", 128, qx, 0, C)
+
         if t == 0:
             ts("km8", ["gn"], T.m8[:], T.ni[:], F(29), ALU.is_equal)
             do("v", "km8", [], V.memset, T.dg[:], 0)
+        else:
+            scores()
         for h in range(2):
             hs = str(h)
             mk_, rmh = T.mk[:, C * h:C * h + C], rm[:, C * h:C * h + C]
             last, sj = rm[:, C * h + C - 1:C * h + C], T.sj[:, C * h:C * h + C]
             do("v", "mk" + hs, ["mc" + hs, "s15"], V.tensor_tensor, mk_, bank[5 + h][:, 0:C], T.s15[:], ALU.add)
             do("v", "rm" + hs, ["mk" + hs], V.tensor_tensor_scan, rmh, mk_, mk_, -1e29, ALU.max, ALU.max)
-            do("s", "ix" + hs, ["rm" + hs], S.activation, sj, rmh, ACT.Sign, bias=last, scale=-1.0, accum_out=T.ix[:, h:h + 1])
-        send([_m(e_on)], ["rm0"], [RemoteDMATransfer(dst_ids=rid["s"], dma_engine_mask=_m(e_on), remote_sem=T.sem["st" + k], srcs=[rm[:, C - 1:C]], dsts=[T["rst" + k][:], T["rst" + k][:]])])
+            act("ix" + hs, ["rm" + hs], sj, rmh, ACT.Sign, bias=last, scale=-1.0, accum_out=T.ix[:, h:h + 1])
+        if t == 0:
+            quant("qwz", ["kwz"], "qc", 0, 128, "ct", 0)
+        else:
+            act("ath", ["mat"], T.ath[:], bank[2][:, 0:C])
+        send([_m(e_on)], ["rm0"], [RemoteDMATransfer(dst_ids=rid[""] + rid["s"], dma_engine_mask=_m(e_on), remote_sem=T.sem["st" + k],
+                                                     srcs=[rm[:, C - 1:C]], dsts=[T["rst" + k][:] for i in range(4)])])
         send([_m(e_off)], ["rm1"], [RemoteDMATransfer(dst_ids=pid, dma_engine_mask=_m(e_off), remote_sem=T.sem["st" + k], srcs=[rm[:, 2 * C - 1:2 * C]],
                                                       dsts=[T["stl" + k][:, 4 * r:4 * r + 1] for d in peers])])
 
@@ -377,7 +416,7 @@ def _rank_program(g, core, T, topo, r, plan):
         spread(1)
         choose(1)
         for what, sm, lb in (("", "pc", "c0c"), ("s", "ps", "c0s")):
-            ms = [_m(e_on[0:4]), _m(e_on[4:8])]
+            ms = [_m(e_on), _m(e_off)]
             send(ms, [lb], [RemoteDMATransfer(dst_ids=[rid[what][i]], dma_engine_mask=ms[i], remote_sem=T.sem[sm + k],
                                               srcs=[u8("ca" + k, what, 32 * codes_to[i][1], 32 * codes_to[i][1] + 64)], dsts=[u8("rp" + k, what, 0, 64)]) for i in range(2)])
         for what, sm, lb in (("", "pc", "c1c"), ("s", "ps", "c1s")):
@@ -389,11 +428,10 @@ def _rank_program(g, core, T, topo, r, plan):
         do("v", "sown", ["rm1"], V.tensor_copy, T["stl" + k][:, 4 * r:4 * r + 1], rm[:, 2 * C - 1:2 * C])
 
         def wishes():
-            mm("ma", ["uac", "uas", "pth", "ls1"], bank[1][:, 0:C], "ua", 0, qx, 0, C)
-            mm("mat", ["s15"], bank[2][:, 0:C], "ua", 128, qx, 0, C)
-            do("s", "ath", ["mat"], S.activation, T.ath[:], bank[2][:, 0:C], ACT.Copy)
             do("v", "wf", ["ma", "ath"], V.tensor_tensor, T.wf[:], bank[1][:, 0:C], T.ath[:], ALU.is_gt)
             do("v", "pr", ["wf", "kht"], V.tensor_tensor, T.pr[:, 0:C], T.wf[:], T.pf[:], ALU.is_gt)
+
+        def offsets():
             quant("qpr", ["pr"], "qpr", 0, 128, "pr", 0)
             mm("ml", ["qpr", "qwl", "ls1"], bank[0][:, 0:128], "qc", 128, "qpr", 0, 128)
             ts("lf", ["ml"], T.lf[:], bank[0][:, 0:96], F(50), ALU.add)
@@ -401,23 +439,25 @@ def _rank_program(g, core, T, topo, r, plan):
 
         if t == 0:
             consts_a()
+            consts_b1()
         else:
             wishes()
         cnt["st" + k] = 8 * 3 + 8 * 4
         wn, so = T.wn, T["stl" + k]
         do("v", "w1", ["st" + k, "sown"], V.tensor_tensor_scan, wn[:, 0:8], so[:, 0:32:4], so[:, 0:32:4], -1e29, ALU.max, ALU.max)
-        ts("w1", ["w1"], wn[:, 8:16], wn[:, 0:8], wn[:, 7:8], ALU.is_lt)
-        ts("w1", [], wn[:, 18:19], wn[:, 7:8], -2.0 ** 50, ALU.is_lt, 256.0, ALU.mult)
+        ts("w1", ["w1"], wn[:, 8:16], wn[:, 0:8], wn[:, 7:8], ALU.is_lt, 32.0, ALU.mult)
+        ts("w1", ["kc"], wn[:, 18:19], wn[:, 7:8], F(32), ALU.is_lt, 256.0, ALU.mult)
         do("v", "w1", ["w1"], V.tensor_reduce, wn[:, 16:17], wn[:, 8:16], AxisListType.X, ALU.add)
-        ts("w1", ["w1", "kc"], wn[:, 17:18], wn[:, 16:17], 32.0, ALU.mult, F(31), ALU.add)
-        ts("w1", ["w1"], wn[:, 19:20], wn[:, 17:18], wn[:, 18:19], ALU.max, F(32), ALU.max)
-        do("v", "w6", ["w1"], V.tensor_copy, T["wr" + k][:, 0:1], wn[:, 19:20])
-        for gg in range(8):
-            dma("q" if gg % 2 == 0 else "s", "tl", ["w6"], T["tl" + k][16 * gg:16 * gg + 16, 0:2], T["wr" + k][32 * mk:32 * mk + 32, 0:1])
+        ts("w1", ["w1", "kwt"], T.wt[:, 0:1], wn[:, 16:17], F(31), ALU.add, wn[:, 18:19], ALU.max)
+        p0 = 32 * mk
+        do("v", "w2", ["w1"], V.transpose, T.wt[p0:p0 + 32, 32:64], T.wt[p0:p0 + 32, 0:32])
+        do("g", "w3", ["w2"], g.partition_broadcast, T.wt[:, 64:96], T.wt[p0:p0 + 1, 32:64], 128)
         if t == 0:
-            consts_b()
-        else:
-            consts_d()
+            consts_b2()
+        do("v", "w1", ["w3"], V.tensor_tensor, T.wt[:, 96:128], T.wt[:, 64:96], T.wm[:], ALU.mult)
+        for i in range(2):
+            do("v", "w4", ["w1"], V.tensor_reduce, wn[:, 20 + i:21 + i], T.wt[:, 96 + i:128:2], AxisListType.X, ALU.add)
+        do("v", "tl", ["w4"], V.tensor_copy, T["tl" + k][:], wn[:, 20:22])
         cnt["pc" + k] = sum(len(_direct(topo, s, r, cs, own)[0]) for s in peers) + 16
         cnt["ps" + k] = sum(len(_direct(topo, s, r, cs, own)[1]) for s in peers) + 16
         win, tq = "land" + k, "tq" + k
@@ -426,28 +466,46 @@ def _rank_program(g, core, T, topo, r, plan):
         pick("t", [], tq, 0, 32, win, 0, 288, "tl" + k, 0, 2)
         for b in range(4):
             mm("mh%d" % b, ["tc", "ts", "Lw"], bank[3 + b][:, 0:128], "wq", 128 * b, tq, 0, 128)
-            if b % 2 == 0:
+            if b != 1:
                 ts("hv", ["mh%d" % b, "kht"], T.ht[:, b:128:4], bank[3 + b][:, 0:32], 0.03125, ALU.mult)
             else:
-                do("s", "hs", ["mh%d" % b, "kht"], S.activation, T.ht[:, b:128:4], bank[3 + b][:, 0:32], ACT.Copy, scale=0.03125)
+                act("hs", ["mh%d" % b, "kht"], T.ht[:, b:128:4], bank[3 + b][:, 0:32], scale=0.03125)
         qh = "qh" + k
         quant("qh", ["hv", "hs"], qh, 0, 128, "ht", 0)
         a = 128 * me + 32 * mk
-        for what, so_, sx in (("", "yco", "ycx"), ("s", "yso", "ysx")):
-            ms = [_m(e_off), _m(e_on)]
-            send(ms, ["qh"], [
-                RemoteDMATransfer(dst_ids=rid[what], dma_engine_mask=ms[1], remote_sem=T.sem[sx + k], srcs=[u8(qh, what, 0, 32)], dsts=[u8("ry" + k, what, 0, 32) for i in range(2)]),
-                RemoteDMATransfer(dst_ids=pid, dma_engine_mask=ms[0], remote_sem=T.sem[so_ + k], srcs=[u8(qh, what, 0, 32)], dsts=[u8("yq" + k, what, a, a + 32) for d in peers])])
+
+        def out(what, e):
+            return RemoteDMATransfer(dst_ids=rid[what], dma_engine_mask=_m(e), remote_sem=T.sem[("ysx" if what else "ycx") + k], srcs=[u8(qh, what, 0, 32)],
+                                     dsts=[u8("ry" + k, what, 0, 32) for i in range(2)])
+
+        def straight(what):
+            return RemoteDMATransfer(dst_ids=pid, dma_engine_mask=_m(e_off), remote_sem=T.sem[("yso" if what else "yco") + k], srcs=[u8(qh, what, 0, 32)],
+                                     dsts=[u8("yq" + k, what, a, a + 32) for d in peers])
+
+        send([_m(e_off + e_on)], ["qh"], [out("", e_off + e_on)])
+        send([_m(e_on), _m(e_off)], [], [out("s", e_on), straight("s")])
+        send([_m(e_off)], [], [straight("")])
+        for what in ("", "s"):
             dma("q", "yown", ["qh"], u8("yq" + k, what, a, a + 32), u8(qh, what, 0, 32))
         if t == 0:
+            consts_b3()
             consts_c()
+            unpackers(0, 0)
+            scores()
+            act("ath", ["mat"], T.ath[:], bank[2][:, 0:C])
+            unpackers(0, 1)
+            unpackers(1)
             wishes()
+            offsets()
+            quant("qe", ["kes"], "qc", 384, 896, "ct", 1536)
         else:
+            offsets()
+            consts_d()
             do("v", "pw", ["pr"], V.tensor_copy, T.ab[:, 0:4 * C:4], T.pr[:, 0:C])
             quant("qpw", ["pw"], "qab", 0, C, "ab", 0)
             mm("mw", ["qpw", "qww"], bank[7][:, 0:C], "qc", 256, "qab", 0, C)
             ts("wlb", ["mw"], T.wlb[0:8, :], bank[7][0:8, 0:C], fc[0:8, 16:17], ALU.add)
-            dma("q", "swl", ["wlb"], T.wl[:], T.wlb[0:8, :])
+            dma("q", "so", ["wlb"], T.wl[:], T.wlb[0:8, :])
         cnt["yco" + k] = cnt["yso" + k] = 24
         cnt["ycx" + k] = cnt["ysx" + k] = 32
         for i, (half, bb, deps) in enumerate(((me, (3, 4, 5, 6), ["qh", "qe", "yown", "yco" + k, "yso" + k]),
@@ -455,25 +513,24 @@ def _rank_program(g, core, T, topo, r, plan):
             for b in range(4):
                 lb = ("mh%d" if i == 0 else "md%d") % b
                 mm(lb, deps, bank[bb[b]][:, 0:128], "qc", 384 + 128 * b, "yq" + k, 128 * half, 128 * half + 128)
-                out = T.yt[:, 512 * half + b:512 * half + 512:4]
-                if b % 2 == 0:
-                    do("v", "yv", [lb], V.tensor_copy, out, bank[bb[b]][:, 0:128])
+                yo = T.yt[:, 512 * half + b:512 * half + 512:4]
+                if b == 1 or (i == 0 and b == 3):
+                    act("ys", [lb], yo, bank[bb[b]][:, 0:128])
                 else:
-                    do("s", "ys", [lb], S.activation, out, bank[bb[b]][:, 0:128], ACT.Copy)
-        step = (1, 3)[t]
+                    do("v", "yv", [lb], V.tensor_copy, yo, bank[bb[b]][:, 0:128])
+        step = (2, 3)[t]
         n = C // step
         for c in range(step):
-            do("v", "xn%d" % c, ["yv", "ys", "off", "qx"], V.tensor_tensor, xn[:, 4 * n * c:4 * n * (c + 1)],
+            do("v", "xn%d" % c, ["yv", "ys", "off"], V.tensor_tensor, xn[:, 4 * n * c:4 * n * (c + 1)],
                T.yt[:, 0:1024].indirect(T.off[:, n // 4 * c:n // 4 * (c + 1)]), x[:, 4 * n * c:4 * n * (c + 1)], ALU.add)
-            if c:
-                quant("qy%d" % (c - 1), ["xn%d" % (c - 1)], "qx2", n * (c - 1), n * c, "x2", 4 * n * (c - 1))
-        quant("qx" if t == 0 else "qy2", ["xn%d" % (step - 1)], "qx%d" % (t + 1), C - n, C, "x%d" % (t + 1), 4 * (C - n))
+            for e in ([c] if t == 0 else [[], [0], [1, 2]][c]):
+                quant(("qx%d", "qy%d")[t] % e, ["xn%d" % e], "qx%d" % (t + 1), n * e, n * (e + 1), "x%d" % (t + 1), 4 * n * e)
 
     for c in range(3):
         a, b = 128 * c, 128 * c + 128
         mm("my%d" % c, ["qy%d" % c, "vq"], bank[3 + c][:, 0:128], "vq", 0, "qx2", a, b)
         if c < 2:
-            do("s", "yo%d" % c, ["my%d" % c], S.activation, T.yo[:, a:b], bank[3 + c][:, 0:128], ACT.Copy)
+            act("yo%d" % c, ["my%d" % c], T.yo[:, a:b], bank[3 + c][:, 0:128])
         else:
             do("v", "yo%d" % c, ["my%d" % c], V.tensor_copy, T.yo[:, a:b], bank[3 + c][:, 0:128])
         dma("q", "so", ["qy%d" % c], T.oc[:, 4 * a:4 * b], T.qx2[:, a:b].bitcast(dt.uint8))

from concourse.bass import DstId, RemoteDMATransfer
from concourse.mybir import dt, AluOpType, ActivationFunctionType, AxisListType

ALU, ACT = AluOpType, ActivationFunctionType
NR = 8
C = 384
BIG = 2.0 ** 30


def _scratch():
    s = {}

    def bf(name, n): s[name] = ("sbuf", [128, n], "bfloat16")
    def f32(name, n): s[name] = ("sbuf", [128, n], "float32")
    def i32(name, n): s[name] = ("sbuf", [128, n], "int32")
    def u16(name, n): s[name] = ("sbuf", [128, n], "uint16")

    def mx(name, n):
        s[name] = ("sbuf", [128, n], "float8_e4m3fn_x4")
        s[name + "s"] = ("sbuf", [128, n], "uint8")

    bf("ut", 512); bf("vt", 512)
    for t in range(3):
        bf("x%d" % t, 4 * C); mx("qx%d" % t, C)
    bf("ab", 4 * C); bf("hc", 1024); bf("zt", 512); bf("z", 1024); bf("ht", 512); bf("pr", 512)
    bf("ct", 3584); bf("yt", 1024); bf("pf", C); bf("wf", C); bf("sj", 2 * C); bf("wzi", 512)
    f32("pth", C); f32("ath", C); f32("s15", C); f32("mk", 2 * C); f32("ix", 2); f32("fc", 64); f32("m8", 8); f32("ni", 8)
    f32("lf", 96); f32("yo", C); f32("wlb", C); f32("mi", 128); f32("fi", 512); f32("gw", 512); f32("et", 1024)
    f32("wn", 32); f32("wt", 128); f32("wm", 32); f32("wi", 32); f32("la", 24)
    i32("ic", 16); i32("jc", 16); i32("mj", 128); i32("lu", 16); i32("ai", 16); i32("dg", 64)
    u16("lup", 24); u16("lua", 16); u16("ls", 16); u16("off", 96)
    mx("uq", 128); mx("up", 384); mx("ua", 256); mx("vq", 128); mx("wq", 512); mx("qab", C); mx("qhc", 256); mx("zq", 128)
    mx("qz", 256); mx("qpr", 128); mx("qc", 896)
    for t in range(2):
        k = str(t)
        f32("rm" + k, 2 * C); f32("stl" + k, 32); f32("rst" + k, 1); u16("tl" + k, 2)
        mx("ca" + k, 128); mx("cb" + k, 128); mx("land" + k, 288); mx("tq" + k, 128); mx("qh" + k, 128); mx("yq" + k, 256)
        mx("rp" + k, 64); mx("ry" + k, 32)
    for b in range(8):
        s["b%d" % b] = ("psum", [128, 512], "float32")
    return s


SCRATCH = _scratch()
_REMOTE = ["st", "pc", "ps", "yco", "yso", "ycx", "ysx"]
_RSEMS = [n + str(t) for t in range(2) for n in _REMOTE] + ["lr"]
SEMAPHORES = _RSEMS + ["c%d" % i for i in range(135)]


def _m(engines):
    return sum(1 << e for e in engines)


def _plan(T, topo):
    cs = list(T.cores)
    par = [0 if r == 0 or topo.may_write(cs[0], cs[r]) else 1 for r in range(NR)]
    own = [[s for s in range(NR) if par[s] == par[r]] for r in range(NR)]
    cross = [[s for s in range(NR) if par[s] != par[r]] for r in range(NR)]
    kk = [own[r].index(r) for r in range(NR)]
    relay = []
    for r in range(NR):
        can = [c for c in topo.cores_of(cs[r]) if c != cs[r] and all(topo.may_write(c, cs[d]) for d in cross[r])]
        near = [c for c in can if topo.die(c) == topo.die(cs[r])]
        far = [c for c in can if topo.die(c) != topo.die(cs[r])]
        a, b = (near, far) if kk[r] % 2 == 0 else (far, near)
        relay.append([(a[0], 0, 0), (b[0], 2, 0), (a[1], 0, 1), (b[1], 2, 1)])
    return cs, par, own, cross, kk, relay


def _dst(topo, d, core):
    rid, pid = topo.addr(d, core)
    return DstId(rid=rid, pnc=pid)


def _direct(topo, r, d, cs, own):
    o = [s for s in own[r] if s != r]
    e = topo.engines(cs[r], cs[d])
    i = o.index(d)
    return (e[0:4], e[4:6], e[6:8])[i], (e[0:2], e[2:4], e[4:8])[i]


def _relay_program(g, core, T, topo, r, first, role, plan):
    cs, par, own, cross, kk, relay = plan
    d0, d1 = cross[r][first], cross[r][first + 1]
    eng = topo.engines(core, cs[d0])
    ids = [_dst(topo, cs[d], core) for d in (d0, d1)]
    loc = [0]
    what = "s" if role else ""

    def u8(v):
        return v if role else v.bitcast(dt.uint8)

    def send(trs, n):
        g.remote_dma_fused(trs, local_sem=T.sem.lr)
        loc[0] += n

    for t in range(2):
        k = str(t)
        sm = T.sem["st" + k]
        g.wait_ge(sm, 8)
        send([RemoteDMATransfer(dst_ids=[ids[role]], dma_engine_mask=_m(eng), remote_sem=sm, srcs=[T["rst" + k][:]], dsts=[T["stl" + k][:, 4 * r:4 * r + 1]])], len(eng))
        sm = T.sem[("ps" if role else "pc") + k]
        g.wait_ge(sm, 8)
        half = [eng[0:4], eng[4:8]]
        send([RemoteDMATransfer(dst_ids=[ids[i]], dma_engine_mask=_m(half[i]), remote_sem=sm, srcs=[u8(T["rp" + k + what][:, 32 * i:32 * i + 32])],
                                dsts=[u8(T["land" + k + what][:, 32 * r:32 * r + 32])]) for i in range(2)], len(eng))
        a = 128 * par[r] + 32 * kk[r]
        sm = T.sem[("ysx" if role else "ycx") + k]
        g.wait_ge(sm, 8 if role else 16)
        d = T["yq" + k + what]
        send([RemoteDMATransfer(dst_ids=ids, dma_engine_mask=_m(eng), remote_sem=sm, srcs=[u8(T["ry" + k + what][:, 0:32])],
                                dsts=[u8(d[:, a:a + 32]), u8(d[:, a:a + 32])])], len(eng))
    g.wait_ge(T.sem.lr, loc[0])


def rank_program(g, core, T, topo):
    plan = _plan(T, topo)
    rank = T.rank_of(core)
    if rank is None:
        for r in range(NR):
            for c, first, role in plan[5][r]:
                if c == core:
                    _relay_program(g, core, T, topo, r, first, role, plan)
        return
    _rank_program(g, core, T, topo, rank, plan)


def _rank_program(g, core, T, topo, r, plan):
    cs, par, own, cross, kk, relay = plan
    me, mk = par[r], kk[r]
    peers = [s for s in own[r] if s != r]
    V, S, P = g.vector, g.scalar, g.tensor
    names, cnt, seen, done = {}, {}, {}, {}
    bank = [T["b%d" % i] for i in range(8)]
    qid = {"g": g, "v": V, "s": S, "p": P, "q": g.sync}

    def sem(label):
        if label in _RSEMS:
            return T.sem[label]
        if label not in names:
            names[label] = "c%d" % len(names)
        return T.sem[names[label]]

    def w(q, *labels):
        for lb in labels:
            n = cnt.get(lb, 0)
            if n and seen.get((q, lb), 0) < n:
                qid[q].wait_ge(sem(lb), n)
                seen[(q, lb)] = n
                done[lb] = max(done.get(lb, 0), n)

    def do(q, label, deps, method, *args, **kw):
        w(q, *deps)
        n = kw.pop("n", 1)
        method(*args, **kw).then_inc(sem(label), n)
        cnt[label] = cnt.get(label, 0) + n

    def dma(q, label, deps, out, in_):
        do(q, label, deps, qid[q].dma_start, out, in_, n=16)

    def ts(label, deps, out, in0, s1, op0, s2=None, op1=None):
        if op1 is None:
            do("v", label, deps, V.tensor_scalar, out, in0, s1, None, op0)
        else:
            do("v", label, deps, V.tensor_scalar, out, in0, s1, s2, op0, op1)

    def mm(label, deps, out, lhs, la, rhs, ra, rb):
        do("p", label, deps, P.matmul_mx, out, T[lhs][:, la:la + 128], T[lhs + "s"][:, la:la + 128], T[rhs][:, ra:rb], T[rhs + "s"][:, ra:rb], True, True)

    def quant(label, deps, out, a, b, tile, ta):
        do("v", label, deps, V.quantize_mx, T[out][:, a:b], T[out + "s"][:, a:b], T[tile][:, ta:ta + 4 * (b - a)])

    def pick(label, deps, out, a, b, win, wa, wb, off, e, f):
        do("v", label + "c", deps, V.tensor_copy, T[out][:, a:b].bitcast(dt.uint32), T[win][:, wa:wb].bitcast(dt.uint32).indirect(T[off][:, e:f]))
        do("s", label + "s", deps, S.activation, T[out + "s"][:, a:b], T[win + "s"][:, wa:wb].indirect(T[off][:, e:f]), ACT.Copy)

    def act(label, deps, out, in_, func=ACT.Copy, **kw):
        do("s", label, deps, S.activation, out, in_, func, **kw)

    def send(masks, deps, trs):
        w("g", *deps)
        g.remote_dma_fused(trs, local_sem=T.sem.lr)
        cnt["lr"] = cnt.get("lr", 0) + sum(bin(m).count("1") for m in masks)

    def u8(name, what, a, b):
        v = T[name + what][:, a:b]
        return v if what else v.bitcast(dt.uint8)

    def iota(label, out, pattern, base, ch, whole=False):
        if whole:
            do("g", label, [], g.iota, out, pattern, base, ch)
        else:
            do("g", label, [], g.iota, out, pattern, base, ch, allow_small_or_imprecise_dtypes=True)

    fc = T.fc

    def F(a, n=1):
        return fc[:, a:a + n]

    dma("q", "Lu", [], T.ut[:], T.u[:])
    dma("s", "Lx0", [], T.x0[:, 0:768], T.x[:, 0:768])
    dma("q", "Lx1", [], T.x0[:, 768:1536], T.x[:, 768:1536])
    dma("q", "Lw", ["Lx0", "Lx1"], T.wqs[:], T.ws[:])
    dma("q", "Lw", [], T.wq[:].bitcast(dt.uint8), T.wc[:])
    dma("q", "Lv", [], T.vt[:], T.v[:])

    iota("gl", T.lu[:], [[1, 2], [0, 8]], 0, 16, True)
    iota("gp", T.ic[:], [[0, 16]], 0, 1, True)
    iota("gm", T.mi[:], [[1, 128]], 0, 0)
    iota("gn", T.ni[:], [[1, 8]], 0, 0)
    iota("gz", T.wzi[:], [[0, 8], [1, 16], [0, 4]], 0, 0)
    iota("kz", T.z[:], [[0, 1024]], 0, 0)
    iota("gf", T.fi[:], [[1, 512]], 0, 0)
    iota("gf", T.wi[:], [[1, 16], [0, 2]], 0, 0)
    iota("gf", T.gw[:], [[1, 32], [0, 4], [-1, 4]], 0, 0)

    do("v", "kzt", [], V.memset, T.zt[:], 0.0)
    for i in range(2):
        act("khm", ["kzt"], T.hc[:, 512 * i:512 * i + 512], T.zt[:])
    for i in range(2):
        act("kab", [], T.ab[:, 512 * i:512 * i + 512], T.zt[:])
    do("v", "kl", [], V.memset, T.lup[:, 16:24], 15)
    ts("kl", ["gl"], T.lu[:], T.lu[:], 113, ALU.bitwise_and)
    do("v", "kl", ["kl"], V.tensor_copy, T.lup[:, 0:16], T.lu[:])

    def jbits(*specs):
        for col, shift, mask in specs:
            out, in0 = T.jc[:, col:col + 1], T.ic[:, 0:1]
            if shift and mask:
                ts("kj", ["gp"], out, in0, shift, ALU.logical_shift_right, mask, ALU.bitwise_and)
            elif shift:
                ts("kj", ["gp"], out, in0, shift, ALU.logical_shift_right)
            else:
                ts("kj", ["gp"], out, in0, mask, ALU.bitwise_and)

    jbits((0, 0, 7), (2, 0, 1), (4, 1, 1), (6, 2, 1), (9, 5, 0), (10, 1, 15))
    do("v", "kf", ["kj"], V.tensor_copy, fc[:, 0:8:2], T.jc[:, 0:8:2])
    do("v", "kf", [], V.tensor_copy, fc[:, 9:11], T.jc[:, 9:11])
    ts("k1", ["kf"], F(24), F(2), -1.0, ALU.mult, 2.0, ALU.add)
    ts("k1", [], F(25), F(4), -3.0, ALU.mult, 4.0, ALU.add)
    ts("k1", [], F(26), F(6), -15.0, ALU.mult, 16.0, ALU.add)
    ts("k1", [], F(29), F(9), 2.0, ALU.mult, F(2), ALU.add)
    ts("k1", [], F(23), F(0), 7.0, ALU.is_equal, 128.0, ALU.mult)
    ts("k1", [], F(57), F(10), -1.0, ALU.mult)
    ts("k1", ["k1"], F(27), F(24), F(25), ALU.mult, F(26), ALU.mult)
    ts("k1", ["k1", "gm"], T.mj[:], T.mi[:], F(27), ALU.mult)
    ts("k1", ["k1"], T.mj[:], T.mj[:], 128, ALU.bitwise_and)
    w("v", "k1", "khm")
    for h in range(2):
        out = T.hc[:, 512 * h:512 * h + 512:4]
        if (me if h else 1 - me):
            ts("k1", [], out, T.mj[:], F(23), ALU.add, -BIG / 128, ALU.mult)
        else:
            ts("k1", [], out, T.mj[:], -BIG / 128, ALU.mult)
    quant("uq", ["Lu"], "uq", 0, 128, "ut", 0)
    pick("up", ["uq", "kl"], "up", 0, 256, "uq", 0, 128, "lup", 0, 16)
    quant("qx0", ["Lx0"], "qx0", 0, 192, "x0", 0)
    quant("qx1", ["Lx1"], "qx0", 192, 384, "x0", 768)
    act("kab", [], T.ab[:, 1024:1536], T.zt[:])
    pick("u5", [], "up", 256, 384, "uq", 0, 128, "lup", 16, 24)
    quant("qhc", ["k1"], "qhc", 0, 256, "hc", 0)
    quant("zq", ["kzt"], "zq", 0, 128, "zt", 0)
    for t in range(2):
        for what in ("", "s"):
            dma("q", "kland", ["zq"], u8("land%d" % t, what, 256, 288), u8("zq", what, 0, 32))
            dma("q", "kland", ["zq"], u8("tq%d" % t, what, 32, 128), u8("zq", what, 32, 128))

    def consts_a():
        jbits((1, 4, 0), (3, 4, 1), (5, 5, 1), (7, 6, 1), (8, 3, 1), (11, 0, 3), (12, 0, 127), (14, 0, 15))
        do("v", "kf", ["kj"], V.tensor_copy, fc[:, 1:8:2], T.jc[:, 1:8:2])
        do("v", "kf", [], V.tensor_copy, F(8), T.jc[:, 8:9])
        do("v", "kf", [], V.tensor_copy, F(11, 2), T.jc[:, 11:13])
        do("v", "kf", [], V.tensor_copy, F(22), T.jc[:, 14:15])
        ts("km8", ["kf"], F(30), F(12), 4.0, ALU.mult)
        ts("kc", [], F(31), F(2), 16.0, ALU.mult, F(10), ALU.add)
        if me == 0 and mk == 0:
            ts("kwt", [], F(15), F(12), 0.0, ALU.is_equal, 2.0 ** 81, ALU.mult)
            ts("kc", ["kwt"], F(32), F(15), -2.0 ** 50, ALU.add)
        else:
            do("v", "kc", [], V.memset, F(32), -2.0 ** 50)
        do("v", "kwt", [], V.memset, T.wt[:, 0:32], 0.0)
        ts("kwt", ["gf"], T.wm[:], T.wi[:], F(22), ALU.is_equal)
        for b in range(4):
            ts("ke0", ["km8"], F((28, 43, 55, 56)[b]), F(30), -1.0, ALU.mult, -float(b), ALU.add)
        do("v", "kht", [], V.memset, T.ht[:], 0.0)
        do("v", "kht", [], V.memset, T.pr[:, 384:512], 0.0)
        unpackers(2)
        unpackers(3)

    def unpackers(b, stage=2):
        e = T.et[:, 512 * (b % 2):512 * (b % 2) + 512]
        if stage != 1:
            act("kes", ["ke0", "gf"], e, T.fi[:], ACT.Abs, bias=F((28, 43, 55, 56)[b]))
        if stage:
            act("kes", ["kes"], T.ct[:, 1536 + 512 * b:2048 + 512 * b], e, ACT.Relu, bias=1.0, scale=-1.0)

    def consts_b1():
        ts("kn", [], F(18, 2), F(2, 2), 1.0, ALU.add)
        ts("kn", [], F(20, 2), F(4, 2), 3.0, ALU.mult, 1.0, ALU.add)
        ts("kn", [], F(13), F(6), 15.0, ALU.mult, 1.0, ALU.add)
        ts("kn", [], F(14), F(7), 15.0, ALU.mult, 1.0, ALU.add)
        ts("kn", [], F(35, 2), F(0, 2), 5.0, ALU.is_ge, 0.5, ALU.mult)
        ts("kn", [], F(37, 2), F(0, 2), 0.0, ALU.is_equal, 15.5, ALU.mult)
        ts("kn", [], F(44), F(0), 2.0, ALU.add)
        ts("kn", [], F(45), F(0), F(1), ALU.not_equal)
        ts("kn", [], F(46), F(8), -1.0, ALU.mult, 1.0, ALU.add)
        ts("kn", [], F(54), F(1), 4.0, ALU.mult)
        ts("kn", [], T.la[:, 0:8], T.ni[:], 16.0, ALU.mult)

    def consts_b2():
        do("v", "kn", ["kn"], V.tensor_tensor, F(33, 2), F(18, 2), F(20, 2), ALU.mult)
        ts("kn", [], F(39, 2), F(35, 2), 0.5, ALU.add)
        ts("kn", [], F(58, 6), T.ni[:, 0:6], F(0), ALU.not_equal, F(44), ALU.mult)
        ts("kn", [], T.wn[:, 30:32], T.ni[:, 6:8], F(0), ALU.not_equal, F(44), ALU.mult)
        ts("kn", [], T.la[:, 16:24], T.la[:, 0:8], 1.0, ALU.add)

    def consts_b3():
        do("v", "kn", ["kn"], V.tensor_tensor, F(16, 2), F(33, 2), F(13, 2), ALU.mult)
        do("v", "kn", [], V.tensor_tensor, T.la[:, 8:14], F(58, 6), T.la[:, 0:6], ALU.add)
        do("v", "kn", [], V.tensor_tensor, T.la[:, 14:16], T.wn[:, 30:32], T.la[:, 6:8], ALU.add)
        do("v", "kn", ["kn"], V.tensor_tensor, F(41, 2), F(39, 2), F(16, 2), ALU.mult)
        ts("kn", [], F(51), F(45), F(16), ALU.mult, F(46), ALU.mult)
        do("v", "kla", [], V.tensor_copy, T.lua[:], T.la[:, 8:24])
        do("v", "kn", ["kn"], V.tensor_tensor, F(47, 2), F(41, 2), F(37, 2), ALU.add)
        ts("kn", ["kn"], F(49), F(47), 4.0, ALU.mult, 1024.0, ALU.add)
        ts("kn", [], F(50), F(48), 4.0, ALU.mult, F(11), ALU.add)
        ts("kn", ["kn"], F(52), F(49), F(45), ALU.mult, 1024.0, ALU.subtract)
        ts("kn", ["kn"], F(53), F(52), F(46), ALU.mult)

    def consts_c():
        pick("ua", ["kla"], "ua", 0, 256, "uq", 0, 128, "lua", 0, 16)
        ts("kw", ["gf", "kn"], T.ct[:, 512:1024], T.gw[:], F(54), ALU.is_equal, F(53), ALU.mult)
        quant("qwl", ["kw"], "qc", 128, 256, "ct", 512)

    def consts_d():
        ts("kv", [], T.ct[:, 1024:1536], T.fi[:], F(54), ALU.is_equal, F(51), ALU.mult)
        quant("qww", ["kv"], "qc", 256, 384, "ct", 1024)
        quant("vq", ["Lv"], "vq", 0, 128, "vt", 0)

    codes_to, scales_to = relay[r][0:2], relay[r][2:4]
    e_off = topo.engines(core, cs[peers[0]])
    e_on = [e for e in topo.engines(core, codes_to[0][0]) if e not in e_off]
    rid = {"": [_dst(topo, c[0], core) for c in codes_to], "s": [_dst(topo, c[0], core) for c in scales_to]}
    pid = [_dst(topo, cs[d], core) for d in peers]

    for t in range(2):
        k = str(t)
        qx, x, xn = "qx" + k, T["x" + k], T["x%d" % (t + 1)]
        rm = T["rm" + k]
        for i in range(2):
            lo, hi = 192 * i, 192 * i + 192
            mm("mpt%d" % i, ["qx%d" % i, "upc", "ups"], bank[(1, 4)[i]][:, 0:192], "up", 128, qx, lo, hi)
            mm("mp%d" % i, [], bank[(0, 3)[i]][:, 0:192], "up", 0, qx, lo, hi)
            act("pth%d" % i, ["mpt%d" % i], T.pth[:, lo:hi], bank[(1, 4)[i]][:, 0:192])
        mm("ms", ["u5c", "u5s"], bank[2][:, 0:C], "up", 256, qx, 0, C)
        act("s15", ["ms"], T.s15[:], bank[2][:, 0:C], scale=1.0 / BIG)
        if t == 0:
            act("kwz", ["gz", "k1"], T.et[:, 0:512], T.wzi[:], ACT.Abs, bias=F(57))
            act("kwz", ["kwz"], T.ct[:, 0:512], T.et[:, 0:512], ACT.Relu, bias=1.0, scale=-1.0)
        for i in range(2):
            lo, hi = 192 * i, 192 * i + 192
            do("v", "pf%d" % i, ["mp%d" % i, "pth%d" % i], V.tensor_tensor, T.pf[:, lo:hi], bank[(0, 3)[i]][:, 0:192], T.pth[:, lo:hi], ALU.is_le)
            if i:
                quant("qab", ["ab"], "qab", 0, 192, "ab", 0)
            ts("ab", ["pf%d" % i, "kab"], T.ab[:, 4 * lo:4 * hi:4], T.pf[:, lo:hi], BIG, ALU.mult)
        quant("qab", ["ab"], "qab", 192, 384, "ab", 768)
        for h in range(2):
            mm("mc%d" % h, ["qab", "qhc"], bank[5 + h][:, 0:C], "qhc", 128 * h, "qab", 0, C)

        def scores():
            mm("ma", ["uac", "uas", "pth0", "pth1"], bank[1][:, 0:C], "ua", 0, qx, 0, C)
            mm("mat", ["s15"], bank[2][:, 0:C], "ua", 128, qx, 0, C)

        if t == 0:
            ts("km8", ["gn"], T.m8[:], T.ni[:], F(29), ALU.is_equal)
            do("v", "km8", [], V.memset, T.dg[:], 0)
        else:
            scores()
        for h in range(2):
            hs = str(h)
            mk_, rmh = T.mk[:, C * h:C * h + C], rm[:, C * h:C * h + C]
            last, sj = rm[:, C * h + C - 1:C * h + C], T.sj[:, C * h:C * h + C]
            do("v", "mk" + hs, ["mc" + hs, "s15"], V.tensor_tensor, mk_, bank[5 + h][:, 0:C], T.s15[:], ALU.add)
            do("v", "rm" + hs, ["mk" + hs], V.tensor_tensor_scan, rmh, mk_, mk_, -1e29, ALU.max, ALU.max)
            act("ix" + hs, ["rm" + hs], sj, rmh, ACT.Sign, bias=last, scale=-1.0, accum_out=T.ix[:, h:h + 1])
        if t == 0:
            quant("qwz", ["kwz"], "qc", 0, 128, "ct", 0)
        else:
            act("ath", ["mat"], T.ath[:], bank[2][:, 0:C])
        send([_m(e_on)], ["rm0"], [RemoteDMATransfer(dst_ids=rid[""] + rid["s"], dma_engine_mask=_m(e_on), remote_sem=T.sem["st" + k],
                                                     srcs=[rm[:, C - 1:C]], dsts=[T["rst" + k][:] for i in range(4)])])
        send([_m(e_off)], ["rm1"], [RemoteDMATransfer(dst_ids=pid, dma_engine_mask=_m(e_off), remote_sem=T.sem["st" + k], srcs=[rm[:, 2 * C - 1:2 * C]],
                                                      dsts=[T["stl" + k][:, 4 * r:4 * r + 1] for d in peers])])

        def digits(h):
            hs, ai = str(h), T.ai[:, 8 * h:8 * h + 8]
            ts("da" + hs, ["ix" + hs, "km8"], ai, T.m8[:], T.ix[:, h:h + 1], ALU.mult)
            for b, ma in enumerate((448, 56, 7)):
                ts("db" + hs, ["da" + hs], T.dg[:, 32 * h + b:32 * h + 32:4], ai, ma, ALU.bitwise_and)

        def spread(h):
            hs = str(h)
            do("v", "dz" + hs, ["db" + hs, "kz"], V.tensor_copy, T.z[:, 512 * h:512 * h + 32], T.dg[:, 32 * h:32 * h + 32])
            quant("qz" + hs, ["dz" + hs], "qz", 128 * h, 128 * h + 128, "z", 512 * h)
            mm("mz" + hs, ["qz" + hs, "qwz"], bank[(7, 0)[h]][:, 0:128], "qc", 0, "qz", 128 * h, 128 * h + 128)

        def choose(h):
            hs = str(h)
            do("v", "ls" + hs, ["mz" + hs], V.tensor_copy, T.ls[:, 8 * h:8 * h + 8], bank[(7, 0)[h]][:, 0:8])
            pick("c" + hs, ["ls" + hs], ("ca", "cb")[h] + k, 0, 128, qx, 0, C, "ls", 8 * h, 8 * h + 8)

        digits(0)
        spread(0)
        digits(1)
        choose(0)
        spread(1)
        choose(1)
        for what, sm, lb in (("", "pc", "c0c"), ("s", "ps", "c0s")):
            ms = [_m(e_on), _m(e_off)]
            send(ms, [lb], [RemoteDMATransfer(dst_ids=[rid[what][i]], dma_engine_mask=ms[i], remote_sem=T.sem[sm + k],
                                              srcs=[u8("ca" + k, what, 32 * codes_to[i][1], 32 * codes_to[i][1] + 64)], dsts=[u8("rp" + k, what, 0, 64)]) for i in range(2)])
        for what, sm, lb in (("", "pc", "c1c"), ("s", "ps", "c1s")):
            ms = [_m(_direct(topo, r, d, cs, own)[1 if what else 0]) for d in peers]
            send(ms, [lb], [RemoteDMATransfer(dst_ids=[pid[i]], dma_engine_mask=ms[i], remote_sem=T.sem[sm + k],
                                              srcs=[u8("cb" + k, what, 32 * kk[d], 32 * kk[d] + 32)], dsts=[u8("land" + k, what, 32 * r, 32 * r + 32)]) for i, d in enumerate(peers)])
        for what, lb in (("", "c1c"), ("s", "c1s")):
            dma("q", "cown" + what, [lb], u8("land" + k, what, 32 * r, 32 * r + 32), u8("cb" + k, what, 32 * mk, 32 * mk + 32))
        do("v", "sown", ["rm1"], V.tensor_copy, T["stl" + k][:, 4 * r:4 * r + 1], rm[:, 2 * C - 1:2 * C])

        def wishes():
            do("v", "wf", ["ma", "ath"], V.tensor_tensor, T.wf[:], bank[1][:, 0:C], T.ath[:], ALU.is_gt)
            do("v", "pr", ["wf", "kht"], V.tensor_tensor, T.pr[:, 0:C], T.wf[:], T.pf[:], ALU.is_gt)

        def offsets():
            quant("qpr", ["pr"], "qpr", 0, 128, "pr", 0)
            mm("ml", ["qpr", "qwl", "ls1"], bank[0][:, 0:128], "qc", 128, "qpr", 0, 128)
            ts("lf", ["ml"], T.lf[:], bank[0][:, 0:96], F(50), ALU.add)
            do("v", "off", ["lf"], V.tensor_copy, T.off[:], T.lf[:])

        if t == 0:
            consts_a()
            consts_b1()
        else:
            wishes()
        cnt["st" + k] = 8 * 3 + 8 * 4
        wn, so = T.wn, T["stl" + k]
        do("v", "w1", ["st" + k, "sown"], V.tensor_tensor_scan, wn[:, 0:8], so[:, 0:32:4], so[:, 0:32:4], -1e29, ALU.max, ALU.max)
        ts("w1", ["w1"], wn[:, 8:16], wn[:, 0:8], wn[:, 7:8], ALU.is_lt, 32.0, ALU.mult)
        ts("w1", ["kc"], wn[:, 18:19], wn[:, 7:8], F(32), ALU.is_lt, 256.0, ALU.mult)
        do("v", "w1", ["w1"], V.tensor_reduce, wn[:, 16:17], wn[:, 8:16], AxisListType.X, ALU.add)
        ts("w1", ["w1", "kwt"], T.wt[:, 0:1], wn[:, 16:17], F(31), ALU.add, wn[:, 18:19], ALU.max)
        p0 = 32 * mk
        do("v", "w2", ["w1"], V.transpose, T.wt[p0:p0 + 32, 32:64], T.wt[p0:p0 + 32, 0:32])
        do("g", "w3", ["w2"], g.partition_broadcast, T.wt[:, 64:96], T.wt[p0:p0 + 1, 32:64], 128)
        if t == 0:
            consts_b2()
        do("v", "w1", ["w3"], V.tensor_tensor, T.wt[:, 96:128], T.wt[:, 64:96], T.wm[:], ALU.mult)
        for i in range(2):
            do("v", "w4", ["w1"], V.tensor_reduce, wn[:, 20 + i:21 + i], T.wt[:, 96 + i:128:2], AxisListType.X, ALU.add)
        do("v", "tl", ["w4"], V.tensor_copy, T["tl" + k][:], wn[:, 20:22])
        cnt["pc" + k] = sum(len(_direct(topo, s, r, cs, own)[0]) for s in peers) + 16
        cnt["ps" + k] = sum(len(_direct(topo, s, r, cs, own)[1]) for s in peers) + 16
        win, tq = "land" + k, "tq" + k
        w("v", "tl", "kland", "cown", "pc" + k)
        w("s", "tl", "kland", "cowns", "ps" + k)
        pick("t", [], tq, 0, 32, win, 0, 288, "tl" + k, 0, 2)
        for b in range(4):
            mm("mh%d" % b, ["tc", "ts", "Lw"], bank[3 + b][:, 0:128], "wq", 128 * b, tq, 0, 128)
            if b != 1:
                ts("hv", ["mh%d" % b, "kht"], T.ht[:, b:128:4], bank[3 + b][:, 0:32], 0.03125, ALU.mult)
            else:
                act("hs", ["mh%d" % b, "kht"], T.ht[:, b:128:4], bank[3 + b][:, 0:32], scale=0.03125)
        qh = "qh" + k
        quant("qh", ["hv", "hs"], qh, 0, 128, "ht", 0)
        a = 128 * me + 32 * mk

        def out(what, e):
            return RemoteDMATransfer(dst_ids=rid[what], dma_engine_mask=_m(e), remote_sem=T.sem[("ysx" if what else "ycx") + k], srcs=[u8(qh, what, 0, 32)],
                                     dsts=[u8("ry" + k, what, 0, 32) for i in range(2)])

        def straight(what):
            return RemoteDMATransfer(dst_ids=pid, dma_engine_mask=_m(e_off), remote_sem=T.sem[("yso" if what else "yco") + k], srcs=[u8(qh, what, 0, 32)],
                                     dsts=[u8("yq" + k, what, a, a + 32) for d in peers])

        send([_m(e_off + e_on)], ["qh"], [out("", e_off + e_on)])
        send([_m(e_on), _m(e_off)], [], [out("s", e_on), straight("s")])
        send([_m(e_off)], [], [straight("")])
        for what in ("", "s"):
            dma("q", "yown", ["qh"], u8("yq" + k, what, a, a + 32), u8(qh, what, 0, 32))
        if t == 0:
            consts_b3()
            consts_c()
            unpackers(0, 0)
            scores()
            act("ath", ["mat"], T.ath[:], bank[2][:, 0:C])
            unpackers(0, 1)
            unpackers(1)
            wishes()
            offsets()
            quant("qe", ["kes"], "qc", 384, 896, "ct", 1536)
        else:
            offsets()
            consts_d()
            do("v", "pw", ["pr"], V.tensor_copy, T.ab[:, 0:4 * C:4], T.pr[:, 0:C])
            quant("qpw", ["pw"], "qab", 0, C, "ab", 0)
            mm("mw", ["qpw", "qww"], bank[7][:, 0:C], "qc", 256, "qab", 0, C)
            ts("wlb", ["mw"], T.wlb[0:8, :], bank[7][0:8, 0:C], fc[0:8, 16:17], ALU.add)
            dma("q", "so", ["wlb"], T.wl[:], T.wlb[0:8, :])
        cnt["yco" + k] = cnt["yso" + k] = 24
        cnt["ycx" + k] = cnt["ysx" + k] = 32
        for i, (half, bb, deps) in enumerate(((me, (3, 4, 5, 6), ["qh", "qe", "yown", "yco" + k, "yso" + k]),
                                              (1 - me, (1, 2, 7, 0), ["wf", "ath", "wlb", "lf", "ls0", "ycx" + k, "ysx" + k]))):
            for b in range(4):
                lb = ("mh%d" if i == 0 else "md%d") % b
                mm(lb, deps, bank[bb[b]][:, 0:128], "qc", 384 + 128 * b, "yq" + k, 128 * half, 128 * half + 128)
                yo = T.yt[:, 512 * half + b:512 * half + 512:4]
                if b == 1 or (i == 0 and b == 3):
                    act("ys", [lb], yo, bank[bb[b]][:, 0:128])
                else:
                    do("v", "yv", [lb], V.tensor_copy, yo, bank[bb[b]][:, 0:128])
        step = (2, 3)[t]
        n = C // step
        for c in range(step):
            do("v", "xn%d" % c, ["yv", "ys", "off"], V.tensor_tensor, xn[:, 4 * n * c:4 * n * (c + 1)],
               T.yt[:, 0:1024].indirect(T.off[:, n // 4 * c:n // 4 * (c + 1)]), x[:, 4 * n * c:4 * n * (c + 1)], ALU.add)
            for e in ([c] if t == 0 else [[], [0], [1, 2]][c]):
                quant(("qx%d", "qy%d")[t] % e, ["xn%d" % e], "qx%d" % (t + 1), n * e, n * (e + 1), "x%d" % (t + 1), 4 * n * e)

    for c in range(3):
        a, b = 128 * c, 128 * c + 128
        mm("my%d" % c, ["qy%d" % c, "vq"], bank[3 + c][:, 0:128], "vq", 0, "qx2", a, b)
        if c < 2:
            act("yo%d" % c, ["my%d" % c], T.yo[:, a:b], bank[3 + c][:, 0:128])
        else:
            do("v", "yo%d" % c, ["my%d" % c], V.tensor_copy, T.yo[:, a:b], bank[3 + c][:, 0:128])
        dma("q", "so", ["qy%d" % c], T.oc[:, 4 * a:4 * b], T.qx2[:, a:b].bitcast(dt.uint8))
        dma("q", "so", ["yo%d" % c], T.y[:, a:b], T.yo[:, a:b])
    for i in range(4):
        dma("s", "ss", ["qy0", "qy1", "qy2"], T.osc[4 * i:4 * i + 4, :], T.qx2s[32 * i:32 * i + 4, :])
    w("s", "ss")
    for lb in list(cnt):
        if done.get(lb, 0) < cnt[lb]:
            w("g" if lb == "lr" else "q", lb)
